import numpy as np
import ml_dtypes


def mxq(x, axis, fmt="e4m3"):
    dtype, down = {"e4m3": (ml_dtypes.float8_e4m3fn, 7), "e5m2": (ml_dtypes.float8_e5m2, 14)}[fmt]
    v = np.moveaxis(np.asarray(x, np.float32).astype(ml_dtypes.bfloat16).astype(np.float64), axis, -1)
    blocks = v.reshape(v.shape[:-1] + (-1, 32))
    amax = np.abs(blocks).max(-1, keepdims=True)
    byte = np.maximum(np.where(amax > 0, np.frexp(amax)[1] - 1 + 127, 0) - down, 1)
    scale = np.exp2(byte - 127.0)
    codes = (blocks / scale).astype(np.float32).astype(dtype).astype(np.float64)
    return np.moveaxis((codes * scale).reshape(v.shape), -1, axis)


WIDE = False


def mx_kscale(k):
    if not WIDE:
        return np.ones(k)
    levels = np.array([10, -10, 5, -5, 0])
    if k % 512:
        return np.exp2(np.random.permutation(np.resize(levels, k // 32))).repeat(32)
    a = np.empty((k // 512, 16))
    for p in range(k // 512):
        a[p, :8] = np.random.permutation(np.resize(levels, 8))
        for g in range(8):
            far = levels[np.abs(levels - a[p, g]) >= 10]
            a[p, g + 8] = far[np.random.randint(len(far))]
    return np.exp2(a.ravel()).repeat(32)


def f64(x):
    return np.asarray(x).astype(np.float64)


def striped(idx):
    return np.tile(idx.reshape(-1, 16).T, (8, 1)).astype(np.uint16)


def unstriped(offs):
    return offs[:16].T.reshape(-1).astype(np.int64)


E2M1 = np.array([0.0, 0.5, 1.0, 1.5, 2.0, 3.0, 4.0, 6.0, -0.0, -0.5, -1.0, -1.5, -2.0, -3.0, -4.0, -6.0])


def pack_weight(w, fmt):
    k, n = w.shape
    w = f64(np.asarray(w, np.float32).astype(ml_dtypes.bfloat16)).reshape(k // 32, 32, n)
    amax = np.abs(w).max(1)
    if fmt == "e4m3":
        byte = np.frexp(amax)[1] - 1 + 127 - 7
    else:
        mant, ex = np.frexp(amax / 6.0)
        byte = np.where(mant > 0.5, ex, ex - 1) + 127
    byte = np.clip(np.where(amax > 0, byte, 1), 1, 254)
    scaled = (w * np.exp2(127.0 - byte)[:, None, :]).reshape(k, n).astype(np.float32)
    by_word = np.ascontiguousarray(scaled.reshape(k // 512, 128, 4, n).transpose(0, 1, 3, 2))
    if fmt == "e4m3":
        words = by_word.astype(ml_dtypes.float8_e4m3fn).view(np.uint8)
    else:
        c = by_word.astype(ml_dtypes.float4_e2m1fn).view(np.uint8) & 0xF
        words = (c[..., 0::2] | (c[..., 1::2] << 4)).reshape(k // 512, 128, 2 * n)
    return np.ascontiguousarray(words), np.ascontiguousarray(byte.astype(np.uint8).reshape(k // 512, 16, n))


def unpack_weight(words, scales, fmt):
    g, _, n = scales.shape
    words = np.ascontiguousarray(words).reshape(g, 128, n, -1)
    if fmt == "e4m3":
        vals = words.view(ml_dtypes.float8_e4m3fn).astype(np.float64)
    else:
        nib = np.empty((g, 128, n, 4), np.uint8)
        nib[..., 0::2] = words & 0xF
        nib[..., 1::2] = words >> 4
        vals = E2M1[nib]
    vals = vals * np.repeat(np.exp2(scales.astype(np.float64) - 127.0), 8, axis=1)[..., None]
    return vals.transpose(0, 1, 3, 2).reshape(g * 512, n)


def silu(v):
    return v / (1.0 + np.exp(-np.maximum(v, -700.0)))


K, T, E, C, N = 2560, 1024, 4, 128, 128
K8 = 1024


def by_expert(wq, xq):
    return np.concatenate([wq[e].T @ xq[:, e * C:(e + 1) * C] for e in range(E)], axis=1)


def setup_inputs():
    n = np.random.standard_normal
    s = mx_kscale(K)[:, None]
    w = n((E, K, N)) / np.sqrt(K) / s[None]
    w8 = [pack_weight(m[:K8], "e4m3") for m in w]
    w4 = [pack_weight(m[K8:], "e2m1") for m in w]
    return {
        "xT": (n((K, T)) * s).astype(np.float32),
        "xr": n((N, T)).astype(np.float32),
        "w8_words": np.stack([m[0] for m in w8]),
        "w8_scales": np.stack([m[1] for m in w8]),
        "w4_words": np.stack([m[0] for m in w4]),
        "w4_scales": np.stack([m[1] for m in w4]),
        "b": (0.3 * n((N, E))).astype(np.float32),
        "gate": np.tile(np.random.uniform(0.2, 1.0, E * C), (N, 1)).astype(np.float32),
        "offs": striped(np.random.permutation(T)[:E * C]),
    }


def reference(xT, xr, w8_words, w8_scales, w4_words, w4_scales, b, gate, offs):
    idx = unstriped(offs)
    w = np.stack([np.concatenate([unpack_weight(w8_words[e], w8_scales[e], "e4m3"), unpack_weight(w4_words[e], w4_scales[e], "e2m1")]) for e in range(E)])
    xq = mxq(f64(xT)[:, idx], 0, "e4m3")
    y = by_expert(w, xq)
    y = silu(y + np.repeat(f64(b), C, axis=1))
    out = f64(xr).copy()
    out[:, idx] += f64(gate) * y
    return out

@@ -1,0 +1,181 @@
+from contextlib import ExitStack
+
+import concourse.mybir as mybir
+
+F32 = mybir.dt.float32
+BF16 = mybir.dt.bfloat16
+U32 = mybir.dt.uint32
+I32 = mybir.dt.int32
+U16 = mybir.dt.uint16
+U8 = mybir.dt.uint8
+FP8X4 = mybir.dt.float8_e4m3fn_x4
+FP4X4 = mybir.dt.float4_e2m1fn_x4
+ACT = mybir.ActivationFunctionType
+ALU = mybir.AluOpType
+
+P = 128
+K, T, E, C, N = 2560, 1024, 4, 128, 128
+PASSES8, PASSES4 = 2, 3
+PASSES = PASSES8 + PASSES4
+SLOTS = E * C
+
+ORDER = ((2, 0, 0), (3, 1, 0), (0, 2, 4), (1, 2, 8), (4, 2, 0))
+SCALE_TILES = 3
+LOADS = (((0, 1024),),) * 4 + (((0, 512), (512, 768), (768, 1024)),)
+UNITS = (
+    (((0, 320, 512), (512, 816, 1024)),),
+    (((0, 320, 512), (512, 704, 1024)),),
+    (((0, 224, 512), (512, 736, 1024)),),
+    (((0, 176, 512), (512, 880, 1024)),),
+    (((0, 192, 512),), ((512, 512, 768),), ((768, 896, 1024),)),
+)
+
+FLOPS = 2 * K * SLOTS * N
+
+
+def tile_moe_res_lin_silu_kernel(
+    tc, xT, xr, w8_words, w8_scales, w4_words, w4_scales, b, gate, offs, out
+):
+    nc = tc.nc
+    with ExitStack() as ctx:
+        keep = ctx.enter_context(tc.tile_pool(name="keep", bufs=1))
+        psum = ctx.enter_context(tc.psum_pool(name="psum", bufs=1))
+
+        offsets = keep.tile([P, SLOTS // 16], U16, name="offsets")
+        raw = [
+            [(lo, hi, keep.tile([P, 4, hi - lo], F32, name=f"raw{i}_{lo}")) for lo, hi in LOADS[i]]
+            for i in range(PASSES)
+        ]
+        grouped = [keep.tile([P, T, 4], BF16, name=f"grouped{g}", align_bytes=64) for g in range(PASSES)]
+        words = [keep.tile([P, T], U32, name=f"words{g}", align_bytes=64) for g in range(PASSES)]
+        scales = [keep.tile([P, T], U8, name=f"scales{g}", align_bytes=64) for g in range(SCALE_TILES)]
+        slot_words = [keep.tile([P, SLOTS], U32, name=f"slot_words{g}", align_bytes=64) for g in range(PASSES)]
+        slot_scales = [keep.tile([P, SLOTS], U8, name=f"slot_scales{g}", align_bytes=64) for g in range(SCALE_TILES)]
+        w8 = keep.tile([P, E * PASSES8, 4 * N], U8, name="w8", align_bytes=64)
+        w4 = keep.tile([P, E * PASSES4, 2 * N], U8, name="w4", align_bytes=64)
+        w8s = keep.tile([P, E * PASSES8, N], U8, name="w8s", align_bytes=64)
+        w4s = keep.tile([P, E * PASSES4, N], U8, name="w4s", align_bytes=64)
+        bias = keep.tile([P, E], F32, name="bias")
+        gates = keep.tile([P, SLOTS], F32, name="gates")
+        residual = keep.tile([P, T], F32, name="residual")
+        y = keep.tile([P, SLOTS], F32, name="y")
+        scattered = keep.tile([P, T], F32, name="scattered")
+        result = keep.tile([P, T], F32, name="result")
+        warm = keep.tile([P, 8], F32, name="warm")
+        warm_out = keep.tile([P, 8], F32, name="warm_out")
+        acc = [psum.tile([P, C], F32, name=f"acc{e}") for e in range(E)]
+
+        nc.vector.memset(warm[:], 0.0)
+        nc.scalar.activation(warm_out[:], warm[:], ACT.Silu)
+        for g in range(SCALE_TILES):
+            nc.vector.memset(scales[g][:].bitcast(I32), 0)
+        nc.gpsimd.memset(w8s[:].bitcast(I32), 0)
+        nc.gpsimd.memset(w4s[:].bitcast(I32), 0)
+        nc.gpsimd.memset(scattered[:], 0.0)
+
+        def load_scales(planes, codes_scales, q):
+            nc.sync.dma_start(
+                planes[32 * q : 32 * q + 4, :, :].bitcast(I32),
+                codes_scales[:, :, 4 * q : 4 * q + 4, :].rearrange("e a q n -> q (e a) n").bitcast(I32),
+            )
+
+        for i in range(PASSES):
+            g = ORDER[i][0]
+            for lo, hi, tile in raw[i]:
+                rows = xT[512 * g : 512 * (g + 1), lo:hi].rearrange("(p j) t -> p j t", j=4)
+                nc.sync.dma_start(tile[:], rows)
+            if i == 0:
+                nc.sync.dma_start(offsets[:], offs)
+                nc.sync.dma_start(bias[:], b)
+                for q in range(4):
+                    load_scales(w8s, w8_scales, q)
+        for q in range(4):
+            load_scales(w4s, w4_scales, q)
+        nc.sync.dma_start(w4[:], w4_words.rearrange("e a p n -> p (e a) n"))
+        nc.sync.dma_start(w8[:], w8_words.rearrange("e a p n r -> p (e a) (n r)"))
+        nc.sync.dma_start(gates[:], gate)
+        nc.sync.dma_start(residual[:], xr)
+
+        def interleave(i, lo, hi, engine):
+            dst = grouped[i][:, lo:hi, :].rearrange("p (c i) t -> p c t i", i=4)
+            first, tile = [(f, t) for f, end, t in raw[i] if f <= lo and hi <= end][0]
+            src = tile[:, :, lo - first : hi - first].rearrange("p t (c i) -> p c t i", i=4)
+            if engine == "scalar":
+                nc.scalar.activation(dst, src, ACT.Copy)
+            else:
+                nc.vector.tensor_copy(dst, src)
+
+        def quantise(i, lo, hi):
+            tile, row = ORDER[i][1:]
+            nc.vector.quantize_mx(
+                out=words[i][:, lo:hi].bitcast(FP8X4),
+                scales=scales[tile][row:P, lo:hi],
+                in_=grouped[i][:, lo:hi, :].rearrange("p t j -> p (t j)"),
+            )
+
+        def gather_words(i, lo, hi):
+            nc.vector.tensor_copy(slot_words[i][:, lo:hi], words[i][:].indirect(offsets[:, lo // 16 : hi // 16]))
+
+        def gather_scales(tile, lo, hi):
+            nc.vector.tensor_copy(slot_scales[tile][:, lo:hi], scales[tile][:].indirect(offsets[:, lo // 16 : hi // 16]))
+
+        def multiply(i, e):
+            g, tile, row = ORDER[i]
+            cols = slice(e * C, (e + 1) * C)
+            if g < PASSES8:
+                lhs = w8[:, e * PASSES8 + g, :].bitcast(FP8X4)
+                lhs_scale = w8s[:, e * PASSES8 + g, :]
+            else:
+                lhs = w4[:, e * PASSES4 + g - PASSES8, :].bitcast(FP4X4)
+                lhs_scale = w4s[:, e * PASSES4 + g - PASSES8, :]
+            nc.tensor.matmul_mx(
+                out=acc[e][:],
+                lhsT=lhs,
+                lhsT_scale=lhs_scale,
+                rhs=slot_words[i][:, cols].bitcast(FP8X4),
+                rhs_scale=slot_scales[tile][row:P, cols],
+                start=(i == 0),
+                stop=(i == PASSES - 1),
+            )
+
+        def scatter(lo, hi):
+            nc.vector.tensor_tensor(
+                scattered[:].indirect(offsets[:, lo // 16 : hi // 16]), y[:, lo:hi], gates[:, lo:hi], ALU.mult
+            )
+
+        members = [[i for i in range(PASSES) if ORDER[i][1] == tile] for tile in range(SCALE_TILES)]
+        for i in range(PASSES):
+            for group in UNITS[i]:
+                for lo, mid, hi in group:
+                    if mid < hi:
+                        interleave(i, mid, hi, "scalar")
+                    if mid > lo:
+                        interleave(i, lo, mid, "vector")
+                if i == PASSES - 1 and group is UNITS[i][0]:
+                    gather_words(i - 1, 0, SLOTS)
+                for lo, mid, hi in group:
+                    quantise(i, lo, hi)
+            if i < PASSES - 2:
+                gather_words(i, 0, SLOTS)
+                tile = ORDER[i][1]
+                if members[tile] == [i]:
+                    gather_scales(tile, 0, SLOTS)
+                    for e in range(E):
+                        multiply(i, e)
+        i = PASSES - 1
+        tile = ORDER[i][1]
+        half = SLOTS // 2
+        for s in range(2):
+            gather_words(i, s * half, (s + 1) * half)
+            gather_scales(tile, s * half, (s + 1) * half)
+            for m in members[tile]:
+                for e in (2 * s, 2 * s + 1):
+                    multiply(m, e)
+            for e in (2 * s, 2 * s + 1):
+                cols = slice(e * C, (e + 1) * C)
+                nc.scalar.activation(y[:, cols], acc[e][:], ACT.Silu, bias=bias[:, e : e + 1])
+        scatter(0, half)
+        scatter(half, SLOTS)
+        for n, (lo, hi) in enumerate(((0, 512), (512, 768), (768, 1024))):
+            nc.vector.tensor_tensor(result[:, lo:hi], scattered[:, lo:hi], residual[:, lo:hi], ALU.add)
+            (nc.sync if n % 2 == 0 else nc.scalar).dma_start(out[:, lo:hi], result[:, lo:hi])

@@ -19,18 +19,13 @@ PASSES8, PASSES4 = 2, 3
 PASSES = PASSES8 + PASSES4
 SLOTS = E * C
 
+FLOPS = 2 * K * SLOTS * N
+
 ORDER = ((2, 0, 0), (3, 1, 0), (0, 2, 4), (1, 2, 8), (4, 2, 0))
 SCALE_TILES = 3
 LOADS = (((0, 1024),),) * 4 + (((0, 512), (512, 768), (768, 1024)),)
-UNITS = (
-    (((0, 320, 512), (512, 816, 1024)),),
-    (((0, 320, 512), (512, 704, 1024)),),
-    (((0, 224, 512), (512, 736, 1024)),),
-    (((0, 176, 512), (512, 880, 1024)),),
-    (((0, 192, 512),), ((512, 512, 768),), ((768, 896, 1024),)),
-)
-
-FLOPS = 2 * K * SLOTS * N
+VECTOR_TOKENS = ((640,), (448,), (256,), (512,), (192, 0, 64))
+QUANT = 512
 
 
 def tile_moe_res_lin_silu_kernel(
@@ -51,12 +46,12 @@ def tile_moe_res_lin_silu_kernel(
         scales = [keep.tile([P, T], U8, name=f"scales{g}", align_bytes=64) for g in range(SCALE_TILES)]
         slot_words = [keep.tile([P, SLOTS], U32, name=f"slot_words{g}", align_bytes=64) for g in range(PASSES)]
         slot_scales = [keep.tile([P, SLOTS], U8, name=f"slot_scales{g}", align_bytes=64) for g in range(SCALE_TILES)]
-        w8 = keep.tile([P, E * PASSES8, 4 * N], U8, name="w8", align_bytes=64)
-        w4 = keep.tile([P, E * PASSES4, 2 * N], U8, name="w4", align_bytes=64)
-        w8s = keep.tile([P, E * PASSES8, N], U8, name="w8s", align_bytes=64)
-        w4s = keep.tile([P, E * PASSES4, N], U8, name="w4s", align_bytes=64)
+        w8 = [keep.tile([P, 2 * PASSES8, 4 * N], U8, name=f"w8_{h}", align_bytes=64) for h in range(2)]
+        w4 = [keep.tile([P, 2 * PASSES4, 2 * N], U8, name=f"w4_{h}", align_bytes=64) for h in range(2)]
+        staged = keep.tile([16, E * PASSES, N], U8, name="staged", align_bytes=64)
+        planes = keep.tile([P, E * PASSES, N], U8, name="planes", align_bytes=64)
         bias = keep.tile([P, E], F32, name="bias")
-        gates = keep.tile([P, SLOTS], F32, name="gates")
+        gates = [keep.tile([P, 2 * C], F32, name=f"gates{h}") for h in range(2)]
         residual = keep.tile([P, T], F32, name="residual")
         y = keep.tile([P, SLOTS], F32, name="y")
         scattered = keep.tile([P, T], F32, name="scattered")
@@ -69,15 +64,8 @@ def tile_moe_res_lin_silu_kernel(
         nc.scalar.activation(warm_out[:], warm[:], ACT.Silu)
         for g in range(SCALE_TILES):
             nc.vector.memset(scales[g][:].bitcast(I32), 0)
-        nc.gpsimd.memset(w8s[:].bitcast(I32), 0)
-        nc.gpsimd.memset(w4s[:].bitcast(I32), 0)
+        nc.gpsimd.memset(planes[:].bitcast(I32), 0)
         nc.gpsimd.memset(scattered[:], 0.0)
-
-        def load_scales(planes, codes_scales, q):
-            nc.sync.dma_start(
-                planes[32 * q : 32 * q + 4, :, :].bitcast(I32),
-                codes_scales[:, :, 4 * q : 4 * q + 4, :].rearrange("e a q n -> q (e a) n").bitcast(I32),
-            )
 
         for i in range(PASSES):
             g = ORDER[i][0]
@@ -85,20 +73,25 @@ def tile_moe_res_lin_silu_kernel(
                 rows = xT[512 * g : 512 * (g + 1), lo:hi].rearrange("(p j) t -> p j t", j=4)
                 nc.sync.dma_start(tile[:], rows)
             if i == 0:
+                nc.sync.dma_start(
+                    staged[:, 0 : E * PASSES8, :].bitcast(I32), w8_scales.rearrange("e a q n -> q (e a) n").bitcast(I32)
+                )
+                nc.sync.dma_start(
+                    staged[:, E * PASSES8 :, :].bitcast(I32), w4_scales.rearrange("e a q n -> q (e a) n").bitcast(I32)
+                )
                 nc.sync.dma_start(offsets[:], offs)
-                nc.sync.dma_start(bias[:], b)
-                for q in range(4):
-                    load_scales(w8s, w8_scales, q)
         for q in range(4):
-            load_scales(w4s, w4_scales, q)
-        nc.sync.dma_start(w4[:], w4_words.rearrange("e a p n -> p (e a) n"))
-        nc.sync.dma_start(w8[:], w8_words.rearrange("e a p n r -> p (e a) (n r)"))
-        nc.sync.dma_start(gates[:], gate)
+            nc.sync.dma_start(planes[32 * q : 32 * q + 4].bitcast(I32), staged[4 * q : 4 * q + 4].bitcast(I32))
+        for h in range(2):
+            nc.sync.dma_start(w4[h][:], w4_words[2 * h : 2 * h + 2].rearrange("e a p n -> p (e a) n"))
+            nc.sync.dma_start(w8[h][:], w8_words[2 * h : 2 * h + 2].rearrange("e a p n r -> p (e a) (n r)"))
+            if h == 0:
+                nc.sync.dma_start(bias[:], b)
+            nc.sync.dma_start(gates[h][:], gate[:, 2 * C * h : 2 * C * (h + 1)])
         nc.sync.dma_start(residual[:], xr)
 
-        def interleave(i, lo, hi, engine):
+        def interleave(i, tile, first, lo, hi, engine):
             dst = grouped[i][:, lo:hi, :].rearrange("p (c i) t -> p c t i", i=4)
-            first, tile = [(f, t) for f, end, t in raw[i] if f <= lo and hi <= end][0]
             src = tile[:, :, lo - first : hi - first].rearrange("p t (c i) -> p c t i", i=4)
             if engine == "scalar":
                 nc.scalar.activation(dst, src, ACT.Copy)
@@ -122,12 +115,13 @@ def tile_moe_res_lin_silu_kernel(
         def multiply(i, e):
             g, tile, row = ORDER[i]
             cols = slice(e * C, (e + 1) * C)
+            h, m = divmod(e, 2)
             if g < PASSES8:
-                lhs = w8[:, e * PASSES8 + g, :].bitcast(FP8X4)
-                lhs_scale = w8s[:, e * PASSES8 + g, :]
+                lhs = w8[h][:, m * PASSES8 + g, :].bitcast(FP8X4)
+                lhs_scale = planes[:, e * PASSES8 + g, :]
             else:
-                lhs = w4[:, e * PASSES4 + g - PASSES8, :].bitcast(FP4X4)
-                lhs_scale = w4s[:, e * PASSES4 + g - PASSES8, :]
+                lhs = w4[h][:, m * PASSES4 + g - PASSES8, :].bitcast(FP4X4)
+                lhs_scale = planes[:, E * PASSES8 + e * PASSES4 + g - PASSES8, :]
             nc.tensor.matmul_mx(
                 out=acc[e][:],
                 lhsT=lhs,
@@ -138,44 +132,43 @@ def tile_moe_res_lin_silu_kernel(
                 stop=(i == PASSES - 1),
             )
 
-        def scatter(lo, hi):
+        def scatter(h):
+            lo, hi = 2 * C * h, 2 * C * (h + 1)
             nc.vector.tensor_tensor(
-                scattered[:].indirect(offsets[:, lo // 16 : hi // 16]), y[:, lo:hi], gates[:, lo:hi], ALU.mult
+                scattered[:].indirect(offsets[:, lo // 16 : hi // 16]), y[:, lo:hi], gates[h][:], ALU.mult
             )
 
-        members = [[i for i in range(PASSES) if ORDER[i][1] == tile] for tile in range(SCALE_TILES)]
         for i in range(PASSES):
-            for group in UNITS[i]:
-                for lo, mid, hi in group:
-                    if mid < hi:
-                        interleave(i, mid, hi, "scalar")
-                    if mid > lo:
-                        interleave(i, lo, mid, "vector")
-                if i == PASSES - 1 and group is UNITS[i][0]:
-                    gather_words(i - 1, 0, SLOTS)
-                for lo, mid, hi in group:
-                    quantise(i, lo, hi)
+            for (lo, hi, tile), share in zip(raw[i], VECTOR_TOKENS[i]):
+                mid = lo + share
+                pieces = [(q, min(q + QUANT, hi)) for q in range(lo, hi, QUANT)]
+                for q_lo, q_hi in pieces:
+                    if q_lo < mid:
+                        interleave(i, tile, lo, q_lo, min(mid, q_hi), "vector")
+                    if mid < q_hi:
+                        interleave(i, tile, lo, max(mid, q_lo), q_hi, "scalar")
+                for q_lo, q_hi in pieces:
+                    quantise(i, q_lo, q_hi)
             if i < PASSES - 2:
                 gather_words(i, 0, SLOTS)
-                tile = ORDER[i][1]
-                if members[tile] == [i]:
-                    gather_scales(tile, 0, SLOTS)
-                    for e in range(E):
-                        multiply(i, e)
-        i = PASSES - 1
-        tile = ORDER[i][1]
-        half = SLOTS // 2
-        for s in range(2):
-            gather_words(i, s * half, (s + 1) * half)
-            gather_scales(tile, s * half, (s + 1) * half)
-            for m in members[tile]:
-                for e in (2 * s, 2 * s + 1):
-                    multiply(m, e)
-            for e in (2 * s, 2 * s + 1):
-                cols = slice(e * C, (e + 1) * C)
-                nc.scalar.activation(y[:, cols], acc[e][:], ACT.Silu, bias=bias[:, e : e + 1])
-        scatter(0, half)
-        scatter(half, SLOTS)
+            if i == PASSES - 2:
+                gather_words(i, 0, 2 * C)
+            if i < 2:
+                gather_scales(i, 0, SLOTS)
+        last = PASSES - 1
+        for h in range(2):
+            lo, hi = 2 * C * h, 2 * C * (h + 1)
+            if h == 1:
+                gather_words(last - 1, lo, hi)
+            gather_scales(2, lo, hi)
+            gather_words(last, lo, hi)
+            for i in range(PASSES):
+                for e in (2 * h, 2 * h + 1):
+                    multiply(i, e)
+            for e in (2 * h, 2 * h + 1):
+                nc.scalar.activation(y[:, e * C : (e + 1) * C], acc[e][:], ACT.Silu, bias=bias[:, e : e + 1])
+        scatter(0)
+        scatter(1)
         for n, (lo, hi) in enumerate(((0, 512), (512, 768), (768, 1024))):
             nc.vector.tensor_tensor(result[:, lo:hi], scattered[:, lo:hi], residual[:, lo:hi], ALU.add)
             (nc.sync if n % 2 == 0 else nc.scalar).dma_start(out[:, lo:hi], result[:, lo:hi])

@@ -1,6 +1,7 @@
 from contextlib import ExitStack
 
 import concourse.mybir as mybir
+from concourse.masks import make_identity
 
 F32 = mybir.dt.float32
 BF16 = mybir.dt.bfloat16
@@ -21,10 +22,10 @@ SLOTS = E * C
 
 FLOPS = 2 * K * SLOTS * N
 
-ORDER = ((2, 0, 0), (3, 1, 0), (0, 2, 4), (1, 2, 8), (4, 2, 0))
-SCALE_TILES = 3
+ORDER = ((2, 0, 0), (3, 0, 4), (0, 1, 4), (1, 1, 8), (4, 1, 0))
+SCALE_TILES = 2
 LOADS = (((0, 1024),),) * 4 + (((0, 512), (512, 768), (768, 1024)),)
-VECTOR_TOKENS = ((640,), (448,), (256,), (512,), (192, 0, 64))
+VECTOR_TOKENS = ((640,), (576,), (384,), (512,), (64, 0, 96))
 QUANT = 512
 
 
@@ -48,23 +49,31 @@ def tile_moe_res_lin_silu_kernel(
         slot_scales = [keep.tile([P, SLOTS], U8, name=f"slot_scales{g}", align_bytes=64) for g in range(SCALE_TILES)]
         w8 = [keep.tile([P, 2 * PASSES8, 4 * N], U8, name=f"w8_{h}", align_bytes=64) for h in range(2)]
         w4 = [keep.tile([P, 2 * PASSES4, 2 * N], U8, name=f"w4_{h}", align_bytes=64) for h in range(2)]
-        staged = keep.tile([16, E * PASSES, N], U8, name="staged", align_bytes=64)
+        moved_scales = keep.tile([P, SLOTS], U8, name="moved_scales", align_bytes=64)
         planes = keep.tile([P, E * PASSES, N], U8, name="planes", align_bytes=64)
         bias = keep.tile([P, E], F32, name="bias")
-        gates = [keep.tile([P, 2 * C], F32, name=f"gates{h}") for h in range(2)]
+        identity = keep.tile([P, P], F32, name="identity")
+        gate_rows = keep.tile([P, C], F32, name="gate_rows")
+        gate_columns = keep.tile([P, E], F32, name="gate_columns")
+        gates = keep.tile([P, SLOTS], F32, name="gates")
         residual = keep.tile([P, T], F32, name="residual")
         y = keep.tile([P, SLOTS], F32, name="y")
         scattered = keep.tile([P, T], F32, name="scattered")
         result = keep.tile([P, T], F32, name="result")
         warm = keep.tile([P, 8], F32, name="warm")
         warm_out = keep.tile([P, 8], F32, name="warm_out")
+        turned = psum.tile([P, P], F32, name="turned")
+        spread = psum.tile([P, SLOTS], F32, name="spread")
         acc = [psum.tile([P, C], F32, name=f"acc{e}") for e in range(E)]
 
+        nc.vector.memset(planes[:].bitcast(I32), 0)
+        nc.vector.memset(gate_rows[:], 0.0)
+        make_identity(nc, identity[:])
         nc.vector.memset(warm[:], 0.0)
         nc.scalar.activation(warm_out[:], warm[:], ACT.Silu)
         for g in range(SCALE_TILES):
             nc.vector.memset(scales[g][:].bitcast(I32), 0)
-        nc.gpsimd.memset(planes[:].bitcast(I32), 0)
+        nc.gpsimd.memset(moved_scales[:].bitcast(I32), 0)
         nc.gpsimd.memset(scattered[:], 0.0)
 
         for i in range(PASSES):
@@ -74,21 +83,39 @@ def tile_moe_res_lin_silu_kernel(
                 nc.sync.dma_start(tile[:], rows)
             if i == 0:
                 nc.sync.dma_start(
-                    staged[:, 0 : E * PASSES8, :].bitcast(I32), w8_scales.rearrange("e a q n -> q (e a) n").bitcast(I32)
+                    planes[0:16, 0 : E * PASSES8, :].bitcast(I32), w8_scales.rearrange("e a q n -> q (e a) n").bitcast(I32)
                 )
                 nc.sync.dma_start(
-                    staged[:, E * PASSES8 :, :].bitcast(I32), w4_scales.rearrange("e a q n -> q (e a) n").bitcast(I32)
+                    planes[0:16, E * PASSES8 :, :].bitcast(I32), w4_scales.rearrange("e a q n -> q (e a) n").bitcast(I32)
                 )
                 nc.sync.dma_start(offsets[:], offs)
-        for q in range(4):
-            nc.sync.dma_start(planes[32 * q : 32 * q + 4].bitcast(I32), staged[4 * q : 4 * q + 4].bitcast(I32))
-        for h in range(2):
+                nc.sync.dma_start(gate_rows[0:E, :], gate[0:1, :].rearrange("o (e c) -> (o e) c", e=E))
+        for q in range(1, 4):
+            nc.sync.dma_start(planes[32 * q : 32 * q + 4].bitcast(I32), planes[4 * q : 4 * q + 4].bitcast(I32))
+
+        def load_weights(h):
             nc.sync.dma_start(w4[h][:], w4_words[2 * h : 2 * h + 2].rearrange("e a p n -> p (e a) n"))
             nc.sync.dma_start(w8[h][:], w8_words[2 * h : 2 * h + 2].rearrange("e a p n r -> p (e a) (n r)"))
-            if h == 0:
-                nc.sync.dma_start(bias[:], b)
-            nc.sync.dma_start(gates[h][:], gate[:, 2 * C * h : 2 * C * (h + 1)])
-        nc.sync.dma_start(residual[:], xr)
+
+        def load_rest():
+            for q in range(4):
+                nc.sync.dma_start(
+                    moved_scales[32 * q : 32 * q + 4, :].bitcast(I32),
+                    slot_scales[0][32 * q + 4 : 32 * q + 8, :].bitcast(I32),
+                )
+            nc.sync.dma_start(bias[:], b)
+            load_weights(1)
+            nc.sync.dma_start(residual[:], xr)
+
+        load_weights(0)
+
+        nc.tensor.transpose(turned[:], gate_rows[:], identity[:])
+        nc.scalar.copy(gate_columns[:], turned[:, 0:E])
+        for e in range(E):
+            nc.tensor.transpose(
+                spread[:, e * C : (e + 1) * C], gate_columns[:, e : e + 1].to_broadcast([P, P]), identity[:]
+            )
+        nc.scalar.copy(gates[:], spread[:])
 
         def interleave(i, tile, first, lo, hi, engine):
             dst = grouped[i][:, lo:hi, :].rearrange("p (c i) t -> p c t i", i=4)
@@ -127,7 +154,7 @@ def tile_moe_res_lin_silu_kernel(
                 lhsT=lhs,
                 lhsT_scale=lhs_scale,
                 rhs=slot_words[i][:, cols].bitcast(FP8X4),
-                rhs_scale=slot_scales[tile][row:P, cols],
+                rhs_scale=moved_scales[:, cols] if i == 1 else slot_scales[tile][row:P, cols],
                 start=(i == 0),
                 stop=(i == PASSES - 1),
             )
@@ -135,13 +162,15 @@ def tile_moe_res_lin_silu_kernel(
         def scatter(h):
             lo, hi = 2 * C * h, 2 * C * (h + 1)
             nc.vector.tensor_tensor(
-                scattered[:].indirect(offsets[:, lo // 16 : hi // 16]), y[:, lo:hi], gates[h][:], ALU.mult
+                scattered[:].indirect(offsets[:, lo // 16 : hi // 16]), y[:, lo:hi], gates[:, lo:hi], ALU.mult
             )
 
         for i in range(PASSES):
             for (lo, hi, tile), share in zip(raw[i], VECTOR_TOKENS[i]):
                 mid = lo + share
                 pieces = [(q, min(q + QUANT, hi)) for q in range(lo, hi, QUANT)]
+                if share < QUANT:
+                    pieces = pieces[::-1]
                 for q_lo, q_hi in pieces:
                     if q_lo < mid:
                         interleave(i, tile, lo, q_lo, min(mid, q_hi), "vector")
@@ -153,14 +182,15 @@ def tile_moe_res_lin_silu_kernel(
                 gather_words(i, 0, SLOTS)
             if i == PASSES - 2:
                 gather_words(i, 0, 2 * C)
-            if i < 2:
-                gather_scales(i, 0, SLOTS)
+            if i == 1:
+                gather_scales(0, 0, SLOTS)
+                load_rest()
         last = PASSES - 1
         for h in range(2):
             lo, hi = 2 * C * h, 2 * C * (h + 1)
             if h == 1:
                 gather_words(last - 1, lo, hi)
-            gather_scales(2, lo, hi)
+            gather_scales(1, lo, hi)
             gather_words(last, lo, hi)
             for i in range(PASSES):
                 for e in (2 * h, 2 * h + 1):

@@ -25,7 +25,7 @@ FLOPS = 2 * K * SLOTS * N
 ORDER = ((2, 0, 0), (3, 0, 4), (0, 1, 4), (1, 1, 8), (4, 1, 0))
 SCALE_TILES = 2
 LOADS = (((0, 1024),),) * 4 + (((0, 512), (512, 768), (768, 1024)),)
-VECTOR_TOKENS = ((640,), (576,), (384,), (512,), (64, 0, 96))
+VECTOR_TOKENS = ((640,), (576,), (384,), (512,), (128, 0, 128))
 QUANT = 512
 
 
@@ -60,8 +60,6 @@ def tile_moe_res_lin_silu_kernel(
         y = keep.tile([P, SLOTS], F32, name="y")
         scattered = keep.tile([P, T], F32, name="scattered")
         result = keep.tile([P, T], F32, name="result")
-        warm = keep.tile([P, 8], F32, name="warm")
-        warm_out = keep.tile([P, 8], F32, name="warm_out")
         turned = psum.tile([P, P], F32, name="turned")
         spread = psum.tile([P, SLOTS], F32, name="spread")
         acc = [psum.tile([P, C], F32, name=f"acc{e}") for e in range(E)]
@@ -69,8 +67,6 @@ def tile_moe_res_lin_silu_kernel(
         nc.vector.memset(planes[:].bitcast(I32), 0)
         nc.vector.memset(gate_rows[:], 0.0)
         make_identity(nc, identity[:])
-        nc.vector.memset(warm[:], 0.0)
-        nc.scalar.activation(warm_out[:], warm[:], ACT.Silu)
         for g in range(SCALE_TILES):
             nc.vector.memset(scales[g][:].bitcast(I32), 0)
         nc.gpsimd.memset(moved_scales[:].bitcast(I32), 0)
@@ -82,14 +78,15 @@ def tile_moe_res_lin_silu_kernel(
                 rows = xT[512 * g : 512 * (g + 1), lo:hi].rearrange("(p j) t -> p j t", j=4)
                 nc.sync.dma_start(tile[:], rows)
             if i == 0:
+                nc.sync.dma_start(offsets[:], offs)
+                nc.sync.dma_start(gate_rows[0:E, :], gate[0:1, :].rearrange("o (e c) -> (o e) c", e=E))
+            if i == 1:
                 nc.sync.dma_start(
                     planes[0:16, 0 : E * PASSES8, :].bitcast(I32), w8_scales.rearrange("e a q n -> q (e a) n").bitcast(I32)
                 )
                 nc.sync.dma_start(
                     planes[0:16, E * PASSES8 :, :].bitcast(I32), w4_scales.rearrange("e a q n -> q (e a) n").bitcast(I32)
                 )
-                nc.sync.dma_start(offsets[:], offs)
-                nc.sync.dma_start(gate_rows[0:E, :], gate[0:1, :].rearrange("o (e c) -> (o e) c", e=E))
         for q in range(1, 4):
             nc.sync.dma_start(planes[32 * q : 32 * q + 4].bitcast(I32), planes[4 * q : 4 * q + 4].bitcast(I32))
 
@@ -121,7 +118,7 @@ def tile_moe_res_lin_silu_kernel(
             dst = grouped[i][:, lo:hi, :].rearrange("p (c i) t -> p c t i", i=4)
             src = tile[:, :, lo - first : hi - first].rearrange("p t (c i) -> p c t i", i=4)
             if engine == "scalar":
-                nc.scalar.activation(dst, src, ACT.Copy)
+                nc.scalar.copy(dst, src)
             else:
                 nc.vector.tensor_copy(dst, src)
 
@@ -139,7 +136,7 @@ def tile_moe_res_lin_silu_kernel(
         def gather_scales(tile, lo, hi):
             nc.vector.tensor_copy(slot_scales[tile][:, lo:hi], scales[tile][:].indirect(offsets[:, lo // 16 : hi // 16]))
 
-        def multiply(i, e):
+        def multiply(i, e, start, stop):
             g, tile, row = ORDER[i]
             cols = slice(e * C, (e + 1) * C)
             h, m = divmod(e, 2)
@@ -155,8 +152,8 @@ def tile_moe_res_lin_silu_kernel(
                 lhsT_scale=lhs_scale,
                 rhs=slot_words[i][:, cols].bitcast(FP8X4),
                 rhs_scale=moved_scales[:, cols] if i == 1 else slot_scales[tile][row:P, cols],
-                start=(i == 0),
-                stop=(i == PASSES - 1),
+                start=start,
+                stop=stop,
             )
 
         def scatter(h):
@@ -168,8 +165,9 @@ def tile_moe_res_lin_silu_kernel(
         for i in range(PASSES):
             for (lo, hi, tile), share in zip(raw[i], VECTOR_TOKENS[i]):
                 mid = lo + share
-                pieces = [(q, min(q + QUANT, hi)) for q in range(lo, hi, QUANT)]
-                if share < QUANT:
+                step = C if hi == T and i == PASSES - 1 else QUANT
+                pieces = [(q, min(q + step, hi)) for q in range(lo, hi, step)]
+                if share < step:
                     pieces = pieces[::-1]
                 for q_lo, q_hi in pieces:
                     if q_lo < mid:
@@ -191,14 +189,18 @@ def tile_moe_res_lin_silu_kernel(
             if h == 1:
                 gather_words(last - 1, lo, hi)
             gather_scales(1, lo, hi)
-            gather_words(last, lo, hi)
-            for i in range(PASSES):
+            for piece in range(lo, hi, C if h == 0 else 2 * C):
+                gather_words(last, piece, piece + (C if h == 0 else 2 * C))
+            early, late = ((0, 2, 3, 1), (last,)) if h == 0 else ((0, 1, last), (2, 3))
+            for i in early:
                 for e in (2 * h, 2 * h + 1):
-                    multiply(i, e)
+                    multiply(i, e, i == 0, False)
             for e in (2 * h, 2 * h + 1):
+                for i in late:
+                    multiply(i, e, False, i == late[-1])
                 nc.scalar.activation(y[:, e * C : (e + 1) * C], acc[e][:], ACT.Silu, bias=bias[:, e : e + 1])
         scatter(0)
         scatter(1)
-        for n, (lo, hi) in enumerate(((0, 512), (512, 768), (768, 1024))):
+        for n, (lo, hi) in enumerate(((0, 512), (512, 896), (896, 1024))):
             nc.vector.tensor_tensor(result[:, lo:hi], scattered[:, lo:hi], residual[:, lo:hi], ALU.add)
             (nc.sync if n % 2 == 0 else nc.scalar).dma_start(out[:, lo:hi], result[:, lo:hi])

@@ -19,14 +19,13 @@ K, T, E, C, N = 2560, 1024, 4, 128, 128
 PASSES8, PASSES4 = 2, 3
 PASSES = PASSES8 + PASSES4
 SLOTS = E * C
+HALVES = 2 * PASSES
 
 FLOPS = 2 * K * SLOTS * N
 
-ORDER = ((2, 0, 0), (3, 0, 4), (0, 1, 4), (1, 1, 8), (4, 1, 0))
-SCALE_TILES = 2
-LOADS = (((0, 1024),),) * 4 + (((0, 512), (512, 768), (768, 1024)),)
-VECTOR_TOKENS = ((640,), (576,), (384,), (512,), (128, 0, 128))
-QUANT = 512
+LOADS = tuple(((0, T, share),) for share in (384, 512, 128, 384, 128, 384, 0, 256, 0)) + (((0, T, 256),),)
+STORES = ((0, 256), (256, 640), (640, 1024))
+SCATTERS = ((0, 128), (128, 256), (256, 512))
 
 
 def tile_moe_res_lin_silu_kernel(
@@ -39,17 +38,15 @@ def tile_moe_res_lin_silu_kernel(
 
         offsets = keep.tile([P, SLOTS // 16], U16, name="offsets")
         raw = [
-            [(lo, hi, keep.tile([P, 4, hi - lo], F32, name=f"raw{i}_{lo}")) for lo, hi in LOADS[i]]
-            for i in range(PASSES)
+            [keep.tile([P, 2, hi - lo], F32, name=f"raw{n}_{lo}") for lo, hi, share in LOADS[n]] for n in range(HALVES)
         ]
-        grouped = [keep.tile([P, T, 4], BF16, name=f"grouped{g}", align_bytes=64) for g in range(PASSES)]
-        words = [keep.tile([P, T], U32, name=f"words{g}", align_bytes=64) for g in range(PASSES)]
-        scales = [keep.tile([P, T], U8, name=f"scales{g}", align_bytes=64) for g in range(SCALE_TILES)]
-        slot_words = [keep.tile([P, SLOTS], U32, name=f"slot_words{g}", align_bytes=64) for g in range(PASSES)]
-        slot_scales = [keep.tile([P, SLOTS], U8, name=f"slot_scales{g}", align_bytes=64) for g in range(SCALE_TILES)]
-        w8 = [keep.tile([P, 2 * PASSES8, 4 * N], U8, name=f"w8_{h}", align_bytes=64) for h in range(2)]
-        w4 = [keep.tile([P, 2 * PASSES4, 2 * N], U8, name=f"w4_{h}", align_bytes=64) for h in range(2)]
-        moved_scales = keep.tile([P, SLOTS], U8, name="moved_scales", align_bytes=64)
+        pairs = [keep.tile([P, 2 * T], BF16, name=f"pairs{n}", align_bytes=64) for n in range(HALVES)]
+        picked = [keep.tile([P, 2, SLOTS], U32, name=f"picked{g}", align_bytes=64) for g in range(PASSES)]
+        woven = [keep.tile([P, 4 * SLOTS], BF16, name=f"woven{g}", align_bytes=64) for g in range(PASSES)]
+        words = [keep.tile([P, SLOTS], U32, name=f"words{g}", align_bytes=64) for g in range(PASSES)]
+        scales = [keep.tile([P, SLOTS], U8, name=f"scales{g}", align_bytes=64) for g in range(PASSES)]
+        w8 = [keep.tile([P, PASSES8, 4 * N], U8, name=f"w8_{e}", align_bytes=64) for e in range(E)]
+        w4 = [keep.tile([P, PASSES4, 2 * N], U8, name=f"w4_{e}", align_bytes=64) for e in range(E)]
         planes = keep.tile([P, E * PASSES, N], U8, name="planes", align_bytes=64)
         bias = keep.tile([P, E], F32, name="bias")
         identity = keep.tile([P, P], F32, name="identity")
@@ -67,44 +64,33 @@ def tile_moe_res_lin_silu_kernel(
         nc.vector.memset(planes[:].bitcast(I32), 0)
         nc.vector.memset(gate_rows[:], 0.0)
         make_identity(nc, identity[:])
-        for g in range(SCALE_TILES):
-            nc.vector.memset(scales[g][:].bitcast(I32), 0)
-        nc.gpsimd.memset(moved_scales[:].bitcast(I32), 0)
         nc.gpsimd.memset(scattered[:], 0.0)
 
-        for i in range(PASSES):
-            g = ORDER[i][0]
-            for lo, hi, tile in raw[i]:
-                rows = xT[512 * g : 512 * (g + 1), lo:hi].rearrange("(p j) t -> p j t", j=4)
-                nc.sync.dma_start(tile[:], rows)
-            if i == 0:
+        for n in range(HALVES):
+            g, u = divmod(n, 2)
+            rows = xT[512 * g : 512 * (g + 1), :].rearrange("(p j) t -> p j t", j=4)
+            for (lo, hi, share), tile in zip(LOADS[n], raw[n]):
+                nc.sync.dma_start(tile[:], rows[:, 2 * u : 2 * u + 2, lo:hi])
+            if n == 0:
                 nc.sync.dma_start(offsets[:], offs)
                 nc.sync.dma_start(gate_rows[0:E, :], gate[0:1, :].rearrange("o (e c) -> (o e) c", e=E))
-            if i == 1:
+            if n == 2:
                 nc.sync.dma_start(
-                    planes[0:16, 0 : E * PASSES8, :].bitcast(I32), w8_scales.rearrange("e a q n -> q (e a) n").bitcast(I32)
+                    planes[0:P:8, 0 : E * PASSES8, :].bitcast(I32),
+                    w8_scales.rearrange("e a q n -> q (e a) n").bitcast(I32),
                 )
                 nc.sync.dma_start(
-                    planes[0:16, E * PASSES8 :, :].bitcast(I32), w4_scales.rearrange("e a q n -> q (e a) n").bitcast(I32)
+                    planes[0:P:8, E * PASSES8 :, :].bitcast(I32),
+                    w4_scales.rearrange("e a q n -> q (e a) n").bitcast(I32),
                 )
-        for q in range(1, 4):
-            nc.sync.dma_start(planes[32 * q : 32 * q + 4].bitcast(I32), planes[4 * q : 4 * q + 4].bitcast(I32))
-
-        def load_weights(h):
-            nc.sync.dma_start(w4[h][:], w4_words[2 * h : 2 * h + 2].rearrange("e a p n -> p (e a) n"))
-            nc.sync.dma_start(w8[h][:], w8_words[2 * h : 2 * h + 2].rearrange("e a p n r -> p (e a) (n r)"))
-
-        def load_rest():
-            for q in range(4):
-                nc.sync.dma_start(
-                    moved_scales[32 * q : 32 * q + 4, :].bitcast(I32),
-                    slot_scales[0][32 * q + 4 : 32 * q + 8, :].bitcast(I32),
-                )
-            nc.sync.dma_start(bias[:], b)
-            load_weights(1)
-            nc.sync.dma_start(residual[:], xr)
-
-        load_weights(0)
+        for r in range(1, 4):
+            nc.sync.dma_start(planes[r:P:32].bitcast(I32), planes[8 * r : P : 32].bitcast(I32))
+        for e in range(E):
+            nc.sync.dma_start(w4[e][:], w4_words[e].rearrange("a p n -> p a n"))
+            nc.sync.dma_start(w8[e][:], w8_words[e].rearrange("a p n r -> p a (n r)"))
+            if e == 0:
+                nc.sync.dma_start(bias[:], b)
+        nc.sync.dma_start(residual[:], xr)
 
         nc.tensor.transpose(turned[:], gate_rows[:], identity[:])
         nc.scalar.copy(gate_columns[:], turned[:, 0:E])
@@ -114,93 +100,80 @@ def tile_moe_res_lin_silu_kernel(
             )
         nc.scalar.copy(gates[:], spread[:])
 
-        def interleave(i, tile, first, lo, hi, engine):
-            dst = grouped[i][:, lo:hi, :].rearrange("p (c i) t -> p c t i", i=4)
-            src = tile[:, :, lo - first : hi - first].rearrange("p t (c i) -> p c t i", i=4)
-            if engine == "scalar":
-                nc.scalar.copy(dst, src)
-            else:
-                nc.vector.tensor_copy(dst, src)
+        def round_pairs(n):
+            for (lo, hi, share), tile in zip(LOADS[n], raw[n]):
+                mid = lo + share
+                for first, last, copy in ((lo, mid, nc.vector.tensor_copy), (mid, hi, nc.scalar.copy)):
+                    if first < last:
+                        copy(
+                            pairs[n][:, 2 * first : 2 * last].rearrange("p (c i j) -> p c j i", i=4, j=2),
+                            tile[:, :, first - lo : last - lo].rearrange("p j (c i) -> p c j i", i=4),
+                        )
 
-        def quantise(i, lo, hi):
-            tile, row = ORDER[i][1:]
-            nc.vector.quantize_mx(
-                out=words[i][:, lo:hi].bitcast(FP8X4),
-                scales=scales[tile][row:P, lo:hi],
-                in_=grouped[i][:, lo:hi, :].rearrange("p t j -> p (t j)"),
+        def gather(n, lo, hi):
+            g, u = divmod(n, 2)
+            nc.vector.tensor_copy(
+                picked[g][:, u, lo:hi], pairs[n][:].bitcast(U32).indirect(offsets[:, lo // 16 : hi // 16])
             )
 
-        def gather_words(i, lo, hi):
-            nc.vector.tensor_copy(slot_words[i][:, lo:hi], words[i][:].indirect(offsets[:, lo // 16 : hi // 16]))
+        def weave(g, lo, hi, on_scalar):
+            dtype = U32 if on_scalar else I32
+            dst = woven[g][:, 4 * lo : 4 * hi].bitcast(dtype).rearrange("p (s u) -> p s u", u=2)
+            src = picked[g][:, :, lo:hi].bitcast(dtype).rearrange("p u s -> p s u")
+            (nc.scalar.copy if on_scalar else nc.vector.tensor_copy)(dst, src)
 
-        def gather_scales(tile, lo, hi):
-            nc.vector.tensor_copy(slot_scales[tile][:, lo:hi], scales[tile][:].indirect(offsets[:, lo // 16 : hi // 16]))
+        def quantise(g, lo, hi):
+            nc.vector.quantize_mx(
+                out=words[g][:, lo:hi].bitcast(FP8X4), scales=scales[g][:, lo:hi], in_=woven[g][:, 4 * lo : 4 * hi]
+            )
 
-        def multiply(i, e, start, stop):
-            g, tile, row = ORDER[i]
+        def multiply(g, e, start, stop):
             cols = slice(e * C, (e + 1) * C)
-            h, m = divmod(e, 2)
             if g < PASSES8:
-                lhs = w8[h][:, m * PASSES8 + g, :].bitcast(FP8X4)
+                lhs = w8[e][:, g, :].bitcast(FP8X4)
                 lhs_scale = planes[:, e * PASSES8 + g, :]
             else:
-                lhs = w4[h][:, m * PASSES4 + g - PASSES8, :].bitcast(FP4X4)
+                lhs = w4[e][:, g - PASSES8, :].bitcast(FP4X4)
                 lhs_scale = planes[:, E * PASSES8 + e * PASSES4 + g - PASSES8, :]
             nc.tensor.matmul_mx(
                 out=acc[e][:],
                 lhsT=lhs,
                 lhsT_scale=lhs_scale,
-                rhs=slot_words[i][:, cols].bitcast(FP8X4),
-                rhs_scale=moved_scales[:, cols] if i == 1 else slot_scales[tile][row:P, cols],
+                rhs=words[g][:, cols].bitcast(FP8X4),
+                rhs_scale=scales[g][:, cols],
                 start=start,
                 stop=stop,
             )
 
-        def scatter(h):
-            lo, hi = 2 * C * h, 2 * C * (h + 1)
+        half = SLOTS // 2
+        for g in range(PASSES - 1):
+            round_pairs(2 * g)
+            gather(2 * g, 0, SLOTS)
+            round_pairs(2 * g + 1)
+            for lo in (0, half):
+                gather(2 * g + 1, lo, lo + half)
+            for lo in (0, half):
+                weave(g, lo, lo + half, False)
+            for lo in (0, half):
+                quantise(g, lo, lo + half)
+        last = PASSES - 1
+        round_pairs(2 * last)
+        gather(2 * last, 0, SLOTS)
+        round_pairs(2 * last + 1)
+        for e in range(E):
+            gather(2 * last + 1, e * C, (e + 1) * C)
+        for e in range(E):
+            weave(last, e * C, (e + 1) * C, True)
+        for e in range(E):
+            quantise(last, e * C, (e + 1) * C)
+        for e in range(E):
+            for n, g in enumerate((2, 3, 0, 1, 4)):
+                multiply(g, e, n == 0, n == PASSES - 1)
+            nc.scalar.activation(y[:, e * C : (e + 1) * C], acc[e][:], ACT.Silu, bias=bias[:, e : e + 1])
+        for lo, hi in SCATTERS:
             nc.vector.tensor_tensor(
                 scattered[:].indirect(offsets[:, lo // 16 : hi // 16]), y[:, lo:hi], gates[:, lo:hi], ALU.mult
             )
-
-        for i in range(PASSES):
-            for (lo, hi, tile), share in zip(raw[i], VECTOR_TOKENS[i]):
-                mid = lo + share
-                step = C if hi == T and i == PASSES - 1 else QUANT
-                pieces = [(q, min(q + step, hi)) for q in range(lo, hi, step)]
-                if share < step:
-                    pieces = pieces[::-1]
-                for q_lo, q_hi in pieces:
-                    if q_lo < mid:
-                        interleave(i, tile, lo, q_lo, min(mid, q_hi), "vector")
-                    if mid < q_hi:
-                        interleave(i, tile, lo, max(mid, q_lo), q_hi, "scalar")
-                for q_lo, q_hi in pieces:
-                    quantise(i, q_lo, q_hi)
-            if i < PASSES - 2:
-                gather_words(i, 0, SLOTS)
-            if i == PASSES - 2:
-                gather_words(i, 0, 2 * C)
-            if i == 1:
-                gather_scales(0, 0, SLOTS)
-                load_rest()
-        last = PASSES - 1
-        for h in range(2):
-            lo, hi = 2 * C * h, 2 * C * (h + 1)
-            if h == 1:
-                gather_words(last - 1, lo, hi)
-            gather_scales(1, lo, hi)
-            for piece in range(lo, hi, C if h == 0 else 2 * C):
-                gather_words(last, piece, piece + (C if h == 0 else 2 * C))
-            early, late = ((0, 2, 3, 1), (last,)) if h == 0 else ((0, 1, last), (2, 3))
-            for i in early:
-                for e in (2 * h, 2 * h + 1):
-                    multiply(i, e, i == 0, False)
-            for e in (2 * h, 2 * h + 1):
-                for i in late:
-                    multiply(i, e, False, i == late[-1])
-                nc.scalar.activation(y[:, e * C : (e + 1) * C], acc[e][:], ACT.Silu, bias=bias[:, e : e + 1])
-        scatter(0)
-        scatter(1)
-        for n, (lo, hi) in enumerate(((0, 512), (512, 896), (896, 1024))):
+        for n, (lo, hi) in enumerate(STORES):
             nc.vector.tensor_tensor(result[:, lo:hi], scattered[:, lo:hi], residual[:, lo:hi], ALU.add)
             (nc.sync if n % 2 == 0 else nc.scalar).dma_start(out[:, lo:hi], result[:, lo:hi])

@@ -23,9 +23,9 @@ HALVES = 2 * PASSES
 
 FLOPS = 2 * K * SLOTS * N
 
-LOADS = tuple(((0, T, share),) for share in (384, 512, 128, 384, 128, 384, 0, 256, 0)) + (((0, T, 256),),)
+LOADS = tuple(((0, T, shares),) for shares in ((448, 256), (256, 384), (0, 448), (256, 384), (0, 448), (256, 384), (0, 448), (256, 384), (0, 448))) + (((0, T, (448, 256)),),)
 STORES = ((0, 256), (256, 640), (640, 1024))
-SCATTERS = ((0, 128), (128, 256), (256, 512))
+SCATTERS = ((0, 256), (256, 512))
 
 
 def tile_moe_res_lin_silu_kernel(
@@ -38,15 +38,25 @@ def tile_moe_res_lin_silu_kernel(
 
         offsets = keep.tile([P, SLOTS // 16], U16, name="offsets")
         raw = [
-            [keep.tile([P, 2, hi - lo], F32, name=f"raw{n}_{lo}") for lo, hi, share in LOADS[n]] for n in range(HALVES)
+            [keep.tile([P, 2, hi - lo], F32, name=f"raw{n}_{lo}", align_bytes=64) for lo, hi, shares in LOADS[n]] for n in range(HALVES)
         ]
         pairs = [keep.tile([P, 2 * T], BF16, name=f"pairs{n}", align_bytes=64) for n in range(HALVES)]
         picked = [keep.tile([P, 2, SLOTS], U32, name=f"picked{g}", align_bytes=64) for g in range(PASSES)]
-        woven = [keep.tile([P, 4 * SLOTS], BF16, name=f"woven{g}", align_bytes=64) for g in range(PASSES)]
-        words = [keep.tile([P, SLOTS], U32, name=f"words{g}", align_bytes=64) for g in range(PASSES)]
+        woven = [
+            keep.tile([P, 4 * SLOTS], BF16, name=f"woven{g}", tag=f"raw{2 * g + 2}_0" if g < PASSES - 1 else "woven", align_bytes=64)
+            for g in range(PASSES)
+        ]
+        reused = {(PASSES - 2, 0): f"raw{HALVES - 1}_{LOADS[-1][-1][0]}", (PASSES - 2, 1): f"pairs{HALVES - 2}"}
+        words = [
+            [
+                keep.tile([P, 2 * C], U32, name=f"words{g}_{h}", tag=reused.get((g, h), f"words{g}_{h}"), align_bytes=64)
+                for h in range(2)
+            ]
+            for g in range(PASSES)
+        ]
         scales = [keep.tile([P, SLOTS], U8, name=f"scales{g}", align_bytes=64) for g in range(PASSES)]
-        w8 = [keep.tile([P, PASSES8, 4 * N], U8, name=f"w8_{e}", align_bytes=64) for e in range(E)]
-        w4 = [keep.tile([P, PASSES4, 2 * N], U8, name=f"w4_{e}", align_bytes=64) for e in range(E)]
+        w8 = [keep.tile([P, 2 * PASSES8, 4 * N], U8, name=f"w8_{h}", align_bytes=64) for h in range(2)]
+        w4 = [keep.tile([P, 2 * PASSES4, 2 * N], U8, name=f"w4_{h}", align_bytes=64) for h in range(2)]
         planes = keep.tile([P, E * PASSES, N], U8, name="planes", align_bytes=64)
         bias = keep.tile([P, E], F32, name="bias")
         identity = keep.tile([P, P], F32, name="identity")
@@ -65,11 +75,13 @@ def tile_moe_res_lin_silu_kernel(
         nc.vector.memset(gate_rows[:], 0.0)
         make_identity(nc, identity[:])
         nc.gpsimd.memset(scattered[:], 0.0)
+        warm = keep.tile([P, 1], F32, name="warm")
+        nc.scalar.activation(warm[:], planes[:, 0, 0:4].bitcast(F32), ACT.Silu)
 
         for n in range(HALVES):
             g, u = divmod(n, 2)
             rows = xT[512 * g : 512 * (g + 1), :].rearrange("(p j) t -> p j t", j=4)
-            for (lo, hi, share), tile in zip(LOADS[n], raw[n]):
+            for (lo, hi, shares), tile in zip(LOADS[n], raw[n]):
                 nc.sync.dma_start(tile[:], rows[:, 2 * u : 2 * u + 2, lo:hi])
             if n == 0:
                 nc.sync.dma_start(offsets[:], offs)
@@ -85,10 +97,10 @@ def tile_moe_res_lin_silu_kernel(
                 )
         for r in range(1, 4):
             nc.sync.dma_start(planes[r:P:32].bitcast(I32), planes[8 * r : P : 32].bitcast(I32))
-        for e in range(E):
-            nc.sync.dma_start(w4[e][:], w4_words[e].rearrange("a p n -> p a n"))
-            nc.sync.dma_start(w8[e][:], w8_words[e].rearrange("a p n r -> p a (n r)"))
-            if e == 0:
+        for h in range(2):
+            nc.sync.dma_start(w4[h][:], w4_words[2 * h : 2 * h + 2].rearrange("e a p n -> p (e a) n"))
+            nc.sync.dma_start(w8[h][:], w8_words[2 * h : 2 * h + 2].rearrange("e a p n r -> p (e a) (n r)"))
+            if h == 0:
                 nc.sync.dma_start(bias[:], b)
         nc.sync.dma_start(residual[:], xr)
 
@@ -100,10 +112,14 @@ def tile_moe_res_lin_silu_kernel(
             )
         nc.scalar.copy(gates[:], spread[:])
 
+        def round_on_gpsimd(dst, src):
+            nc.gpsimd.tensor_scalar(dst, src, 1.0, 0.0, ALU.mult, ALU.add)
+
         def round_pairs(n):
-            for (lo, hi, share), tile in zip(LOADS[n], raw[n]):
-                mid = lo + share
-                for first, last, copy in ((lo, mid, nc.vector.tensor_copy), (mid, hi, nc.scalar.copy)):
+            for (lo, hi, shares), tile in zip(LOADS[n], raw[n]):
+                on_vector, on_gpsimd = shares
+                cuts = (lo, lo + on_vector, lo + on_vector + on_gpsimd, hi)
+                for first, last, copy in zip(cuts, cuts[1:], (nc.vector.tensor_copy, round_on_gpsimd, nc.scalar.copy)):
                     if first < last:
                         copy(
                             pairs[n][:, 2 * first : 2 * last].rearrange("p (c i j) -> p c j i", i=4, j=2),
@@ -124,52 +140,57 @@ def tile_moe_res_lin_silu_kernel(
 
         def quantise(g, lo, hi):
             nc.vector.quantize_mx(
-                out=words[g][:, lo:hi].bitcast(FP8X4), scales=scales[g][:, lo:hi], in_=woven[g][:, 4 * lo : 4 * hi]
+                out=words[g][lo // (2 * C)][:, lo % (2 * C) : (hi - 1) % (2 * C) + 1].bitcast(FP8X4), scales=scales[g][:, lo:hi], in_=woven[g][:, 4 * lo : 4 * hi]
             )
 
         def multiply(g, e, start, stop):
             cols = slice(e * C, (e + 1) * C)
             if g < PASSES8:
-                lhs = w8[e][:, g, :].bitcast(FP8X4)
+                lhs = w8[e // 2][:, e % 2 * PASSES8 + g, :].bitcast(FP8X4)
                 lhs_scale = planes[:, e * PASSES8 + g, :]
             else:
-                lhs = w4[e][:, g - PASSES8, :].bitcast(FP4X4)
+                lhs = w4[e // 2][:, e % 2 * PASSES4 + g - PASSES8, :].bitcast(FP4X4)
                 lhs_scale = planes[:, E * PASSES8 + e * PASSES4 + g - PASSES8, :]
             nc.tensor.matmul_mx(
                 out=acc[e][:],
                 lhsT=lhs,
                 lhsT_scale=lhs_scale,
-                rhs=words[g][:, cols].bitcast(FP8X4),
+                rhs=words[g][e // 2][:, e % 2 * C : (e % 2 + 1) * C].bitcast(FP8X4),
                 rhs_scale=scales[g][:, cols],
                 start=start,
                 stop=stop,
             )
 
         half = SLOTS // 2
-        for g in range(PASSES - 1):
-            round_pairs(2 * g)
-            gather(2 * g, 0, SLOTS)
-            round_pairs(2 * g + 1)
-            for lo in (0, half):
-                gather(2 * g + 1, lo, lo + half)
-            for lo in (0, half):
-                weave(g, lo, lo + half, False)
-            for lo in (0, half):
-                quantise(g, lo, lo + half)
         last = PASSES - 1
-        round_pairs(2 * last)
-        gather(2 * last, 0, SLOTS)
-        round_pairs(2 * last + 1)
+        for g in range(PASSES):
+            round_pairs(2 * g)
+            if g > 0:
+                for lo in (0, half):
+                    weave(g - 1, lo, lo + half, True)
+            gather(2 * g, 0, SLOTS)
+            if 0 < g < last:
+                for lo in (0, half):
+                    quantise(g - 1, lo, lo + half)
+            round_pairs(2 * g + 1)
+            if g < last:
+                gather(2 * g + 1, 0, SLOTS)
         for e in range(E):
             gather(2 * last + 1, e * C, (e + 1) * C)
         for e in range(E):
             weave(last, e * C, (e + 1) * C, True)
-        for e in range(E):
-            quantise(last, e * C, (e + 1) * C)
-        for e in range(E):
-            for n, g in enumerate((2, 3, 0, 1, 4)):
-                multiply(g, e, n == 0, n == PASSES - 1)
-            nc.scalar.activation(y[:, e * C : (e + 1) * C], acc[e][:], ACT.Silu, bias=bias[:, e : e + 1])
+        for lo in (0, half):
+            quantise(last - 1, lo, lo + half)
+            for e in range(lo // C, (lo + half) // C):
+                quantise(last, e * C, (e + 1) * C)
+        for h in range(2):
+            for g in (2, 0, 1):
+                for e in (2 * h, 2 * h + 1):
+                    multiply(g, e, g == 2, False)
+            for e in (2 * h, 2 * h + 1):
+                for g in (last - 1, last):
+                    multiply(g, e, False, g == last)
+                nc.scalar.activation(y[:, e * C : (e + 1) * C], acc[e][:], ACT.Silu, bias=bias[:, e : e + 1])
         for lo, hi in SCATTERS:
             nc.vector.tensor_tensor(
                 scattered[:].indirect(offsets[:, lo // 16 : hi // 16]), y[:, lo:hi], gates[:, lo:hi], ALU.mult

@@ -23,7 +23,7 @@ HALVES = 2 * PASSES
 
 FLOPS = 2 * K * SLOTS * N
 
-LOADS = tuple(((0, T, shares),) for shares in ((448, 256), (256, 384), (0, 448), (256, 384), (0, 448), (256, 384), (0, 448), (256, 384), (0, 448))) + (((0, T, (448, 256)),),)
+LOADS = tuple(((0, T, shares),) for shares in ((448, 256), (384, 256), (0, 352), (0, 448), (0, 352), (0, 448), (0, 352), (0, 448), (0, 352))) + (((0, 704, (0, 352)), (704, T, (0, 0)),),)
 STORES = ((0, 256), (256, 640), (640, 1024))
 SCATTERS = ((0, 256), (256, 512))
 
@@ -43,10 +43,18 @@ def tile_moe_res_lin_silu_kernel(
         pairs = [keep.tile([P, 2 * T], BF16, name=f"pairs{n}", align_bytes=64) for n in range(HALVES)]
         picked = [keep.tile([P, 2, SLOTS], U32, name=f"picked{g}", align_bytes=64) for g in range(PASSES)]
         woven = [
-            keep.tile([P, 4 * SLOTS], BF16, name=f"woven{g}", tag=f"raw{2 * g + 2}_0" if g < PASSES - 1 else "woven", align_bytes=64)
-            for g in range(PASSES)
+            keep.tile([P, 4 * SLOTS], BF16, name=f"woven{g}", tag=f"raw{2 * g + 2}_0" if g < PASSES - 2 else f"raw{HALVES - 1}_{LOADS[-1][-1][0]}", align_bytes=64)
+            for g in range(PASSES - 1)
         ]
-        reused = {(PASSES - 2, 0): f"raw{HALVES - 1}_{LOADS[-1][-1][0]}", (PASSES - 2, 1): f"pairs{HALVES - 2}"}
+        woven_early = [keep.tile([P, 2 * SLOTS], BF16, name=f"woven_early{g}", align_bytes=64) for g in range(PASSES - 1)]
+        woven_last = [keep.tile([P, 4 * C], BF16, name=f"woven_last{e}", align_bytes=64) for e in range(E)]
+
+        def woven_part(g, lo, hi):
+            if g < PASSES - 1 and lo < 2 * C:
+                return woven_early[g][:, 4 * lo : 4 * hi]
+            return woven[g][:, 4 * lo : 4 * hi] if g < PASSES - 1 else woven_last[lo // C][:]
+
+        reused = {(PASSES - 2, 0): "words3_0", (PASSES - 2, 1): "woven_last0"}
         words = [
             [
                 keep.tile([P, 2 * C], U32, name=f"words{g}_{h}", tag=reused.get((g, h), f"words{g}_{h}"), align_bytes=64)
@@ -134,13 +142,13 @@ def tile_moe_res_lin_silu_kernel(
 
         def weave(g, lo, hi, on_scalar):
             dtype = U32 if on_scalar else I32
-            dst = woven[g][:, 4 * lo : 4 * hi].bitcast(dtype).rearrange("p (s u) -> p s u", u=2)
+            dst = woven_part(g, lo, hi).bitcast(dtype).rearrange("p (s u) -> p s u", u=2)
             src = picked[g][:, :, lo:hi].bitcast(dtype).rearrange("p u s -> p s u")
             (nc.scalar.copy if on_scalar else nc.vector.tensor_copy)(dst, src)
 
         def quantise(g, lo, hi):
             nc.vector.quantize_mx(
-                out=words[g][lo // (2 * C)][:, lo % (2 * C) : (hi - 1) % (2 * C) + 1].bitcast(FP8X4), scales=scales[g][:, lo:hi], in_=woven[g][:, 4 * lo : 4 * hi]
+                out=words[g][lo // (2 * C)][:, lo % (2 * C) : (hi - 1) % (2 * C) + 1].bitcast(FP8X4), scales=scales[g][:, lo:hi], in_=woven_part(g, lo, hi)
             )
 
         def multiply(g, e, start, stop):
@@ -166,30 +174,37 @@ def tile_moe_res_lin_silu_kernel(
         for g in range(PASSES):
             round_pairs(2 * g)
             if g > 0:
-                for lo in (0, half):
-                    weave(g - 1, lo, lo + half, True)
+                for lo in (0, C):
+                    weave(g - 1, lo, lo + C, False)
+                for lo in (0, C):
+                    quantise(g - 1, lo, lo + C)
+                if g < last:
+                    weave(g - 1, half, SLOTS, True)
             gather(2 * g, 0, SLOTS)
             if 0 < g < last:
-                for lo in (0, half):
-                    quantise(g - 1, lo, lo + half)
+                quantise(g - 1, half, SLOTS)
             round_pairs(2 * g + 1)
             if g < last:
-                gather(2 * g + 1, 0, SLOTS)
+                for lo in (0, half):
+                    gather(2 * g + 1, lo, lo + half)
+        weave(last - 1, half, SLOTS, True)
         for e in range(E):
             gather(2 * last + 1, e * C, (e + 1) * C)
         for e in range(E):
             weave(last, e * C, (e + 1) * C, True)
-        for lo in (0, half):
-            quantise(last - 1, lo, lo + half)
-            for e in range(lo // C, (lo + half) // C):
-                quantise(last, e * C, (e + 1) * C)
+        for e in range(E):
+            if e == 2:
+                quantise(last - 1, half, SLOTS)
+            quantise(last, e * C, (e + 1) * C)
         for h in range(2):
-            for g in (2, 0, 1):
+            early = (2, 0, 1, last - 1) if h == 0 else (last - 1, 2)
+            late = (last,) if h == 0 else (last, 0, 1)
+            for g in early:
                 for e in (2 * h, 2 * h + 1):
-                    multiply(g, e, g == 2, False)
+                    multiply(g, e, g == early[0], False)
             for e in (2 * h, 2 * h + 1):
-                for g in (last - 1, last):
-                    multiply(g, e, False, g == last)
+                for g in late:
+                    multiply(g, e, False, g == late[-1])
                 nc.scalar.activation(y[:, e * C : (e + 1) * C], acc[e][:], ACT.Silu, bias=bias[:, e : e + 1])
         for lo, hi in SCATTERS:
             nc.vector.tensor_tensor(

@@ -19,11 +19,13 @@ K, T, E, C, N = 2560, 1024, 4, 128, 128
 PASSES8, PASSES4 = 2, 3
 PASSES = PASSES8 + PASSES4
 SLOTS = E * C
-HALVES = 2 * PASSES
+HALF = SLOTS // 2
+LAST = PASSES - 1
 
 FLOPS = 2 * K * SLOTS * N
 
-LOADS = tuple(((0, T, shares),) for shares in ((448, 256), (384, 256), (0, 352), (0, 448), (0, 352), (0, 448), (0, 352), (0, 448), (0, 352))) + (((0, 704, (0, 352)), (704, T, (0, 0)),),)
+LOADS = (((0, 2), (2, 4)), ((0, 2), (2, 4)), ((0, 2), (2, 4)), ((0, 2), (2, 3), (3, 4)), ((0, 1), (1, 2), (2, 3), (3, 4)))
+ORDER = ((2, 3, 0, 1, 4), (2, 3, 0, 1, 4), (4, 2, 3, 0, 1), (4, 2, 3, 0, 1))
 STORES = ((0, 256), (256, 640), (640, 1024))
 SCATTERS = ((0, 256), (256, 512))
 
@@ -37,27 +39,28 @@ def tile_moe_res_lin_silu_kernel(
         psum = ctx.enter_context(tc.psum_pool(name="psum", bufs=1))
 
         offsets = keep.tile([P, SLOTS // 16], U16, name="offsets")
-        raw = [
-            [keep.tile([P, 2, hi - lo], F32, name=f"raw{n}_{lo}", align_bytes=64) for lo, hi, shares in LOADS[n]] for n in range(HALVES)
-        ]
-        pairs = [keep.tile([P, 2 * T], BF16, name=f"pairs{n}", align_bytes=64) for n in range(HALVES)]
-        picked = [keep.tile([P, 2, SLOTS], U32, name=f"picked{g}", align_bytes=64) for g in range(PASSES)]
+        raw = [[keep.tile([P, hi - lo, T], F32, name=f"raw{g}_{lo}", align_bytes=64) for lo, hi in LOADS[g]] for g in range(PASSES)]
+        picked = [keep.tile([P, 4, SLOTS], F32, name=f"picked{g}") for g in range(PASSES)]
         woven = [
-            keep.tile([P, 4 * SLOTS], BF16, name=f"woven{g}", tag=f"raw{2 * g + 2}_0" if g < PASSES - 2 else f"raw{HALVES - 1}_{LOADS[-1][-1][0]}", align_bytes=64)
-            for g in range(PASSES - 1)
+            [keep.tile([P, 4 * HALF], BF16, name=f"woven{g}_{h}", tag=f"woven{g}" if g < LAST - 1 else f"woven{g}_{h}", align_bytes=64) for h in range(2)]
+            for g in range(LAST)
         ]
-        woven_early = [keep.tile([P, 2 * SLOTS], BF16, name=f"woven_early{g}", align_bytes=64) for g in range(PASSES - 1)]
         woven_last = [keep.tile([P, 4 * C], BF16, name=f"woven_last{e}", align_bytes=64) for e in range(E)]
 
-        def woven_part(g, lo, hi):
-            if g < PASSES - 1 and lo < 2 * C:
-                return woven_early[g][:, 4 * lo : 4 * hi]
-            return woven[g][:, 4 * lo : 4 * hi] if g < PASSES - 1 else woven_last[lo // C][:]
+        def interleaved(g, lo, hi):
+            if g == LAST:
+                return woven_last[lo // C][:]
+            return woven[g][lo // HALF][:, 4 * (lo % HALF) : 4 * (lo % HALF + hi - lo)]
 
-        reused = {(PASSES - 2, 0): "words3_0", (PASSES - 2, 1): "woven_last0"}
         words = [
             [
-                keep.tile([P, 2 * C], U32, name=f"words{g}_{h}", tag=reused.get((g, h), f"words{g}_{h}"), align_bytes=64)
+                keep.tile(
+                    [P, HALF],
+                    U32,
+                    name=f"words{g}_{h}",
+                    tag=f"raw{g + 1}_{LOADS[g + 1][-1][0]}" if h == 1 and g < LAST - 1 else f"words{g}_{h}",
+                    align_bytes=64,
+                )
                 for h in range(2)
             ]
             for g in range(PASSES)
@@ -66,6 +69,7 @@ def tile_moe_res_lin_silu_kernel(
         w8 = [keep.tile([P, 2 * PASSES8, 4 * N], U8, name=f"w8_{h}", align_bytes=64) for h in range(2)]
         w4 = [keep.tile([P, 2 * PASSES4, 2 * N], U8, name=f"w4_{h}", align_bytes=64) for h in range(2)]
         planes = keep.tile([P, E * PASSES, N], U8, name="planes", align_bytes=64)
+        staged = keep.tile([P, E * PASSES, N], U8, name="staged", align_bytes=64)
         bias = keep.tile([P, E], F32, name="bias")
         identity = keep.tile([P, P], F32, name="identity")
         gate_rows = keep.tile([P, C], F32, name="gate_rows")
@@ -79,37 +83,32 @@ def tile_moe_res_lin_silu_kernel(
         spread = psum.tile([P, SLOTS], F32, name="spread")
         acc = [psum.tile([P, C], F32, name=f"acc{e}") for e in range(E)]
 
+        nc.scalar.dma_start(
+            staged[0:P:8, 0 : E * PASSES8, :].bitcast(I32), w8_scales.rearrange("e a q n -> q (e a) n").bitcast(I32)
+        )
+        nc.scalar.dma_start(
+            staged[0:P:8, E * PASSES8 :, :].bitcast(I32), w4_scales.rearrange("e a q n -> q (e a) n").bitcast(I32)
+        )
         nc.vector.memset(planes[:].bitcast(I32), 0)
+        nc.gpsimd.dma_start(bias[:], b)
         nc.vector.memset(gate_rows[:], 0.0)
         make_identity(nc, identity[:])
-        nc.gpsimd.memset(scattered[:], 0.0)
+        nc.vector.memset(scattered[:], 0.0)
+        for r in range(4):
+            nc.gpsimd.dma_start(planes[r:P:32].bitcast(I32), staged[8 * r : P : 32].bitcast(I32))
         warm = keep.tile([P, 1], F32, name="warm")
-        nc.scalar.activation(warm[:], planes[:, 0, 0:4].bitcast(F32), ACT.Silu)
+        nc.scalar.activation(warm[:], gate_rows[:, 0:1], ACT.Silu)
 
-        for n in range(HALVES):
-            g, u = divmod(n, 2)
+        for g in range(PASSES):
             rows = xT[512 * g : 512 * (g + 1), :].rearrange("(p j) t -> p j t", j=4)
-            for (lo, hi, shares), tile in zip(LOADS[n], raw[n]):
-                nc.sync.dma_start(tile[:], rows[:, 2 * u : 2 * u + 2, lo:hi])
-            if n == 0:
-                nc.sync.dma_start(offsets[:], offs)
-                nc.sync.dma_start(gate_rows[0:E, :], gate[0:1, :].rearrange("o (e c) -> (o e) c", e=E))
-            if n == 2:
-                nc.sync.dma_start(
-                    planes[0:P:8, 0 : E * PASSES8, :].bitcast(I32),
-                    w8_scales.rearrange("e a q n -> q (e a) n").bitcast(I32),
-                )
-                nc.sync.dma_start(
-                    planes[0:P:8, E * PASSES8 :, :].bitcast(I32),
-                    w4_scales.rearrange("e a q n -> q (e a) n").bitcast(I32),
-                )
-        for r in range(1, 4):
-            nc.sync.dma_start(planes[r:P:32].bitcast(I32), planes[8 * r : P : 32].bitcast(I32))
+            for (lo, hi), tile in zip(LOADS[g], raw[g]):
+                nc.sync.dma_start(tile[:], rows[:, lo:hi, :])
+                if g == 0 and lo == 0:
+                    nc.sync.dma_start(offsets[:], offs)
+                    nc.sync.dma_start(gate_rows[0:E, :], gate[0:1, :].rearrange("o (e c) -> (o e) c", e=E))
         for h in range(2):
             nc.sync.dma_start(w4[h][:], w4_words[2 * h : 2 * h + 2].rearrange("e a p n -> p (e a) n"))
             nc.sync.dma_start(w8[h][:], w8_words[2 * h : 2 * h + 2].rearrange("e a p n r -> p (e a) (n r)"))
-            if h == 0:
-                nc.sync.dma_start(bias[:], b)
         nc.sync.dma_start(residual[:], xr)
 
         nc.tensor.transpose(turned[:], gate_rows[:], identity[:])
@@ -120,38 +119,39 @@ def tile_moe_res_lin_silu_kernel(
             )
         nc.scalar.copy(gates[:], spread[:])
 
-        def round_on_gpsimd(dst, src):
-            nc.gpsimd.tensor_scalar(dst, src, 1.0, 0.0, ALU.mult, ALU.add)
+        def gather(g, j, lo, hi, on_scalar):
+            n = [first <= j < last for first, last in LOADS[g]].index(True)
+            window = raw[g][n][:, j - LOADS[g][n][0], :].indirect(offsets[:, lo // 16 : hi // 16])
+            if on_scalar:
+                nc.scalar.activation(picked[g][:, j, lo:hi], window, ACT.Copy)
+            else:
+                nc.vector.tensor_copy(picked[g][:, j, lo:hi], window)
 
-        def round_pairs(n):
-            for (lo, hi, shares), tile in zip(LOADS[n], raw[n]):
-                on_vector, on_gpsimd = shares
-                cuts = (lo, lo + on_vector, lo + on_vector + on_gpsimd, hi)
-                for first, last, copy in zip(cuts, cuts[1:], (nc.vector.tensor_copy, round_on_gpsimd, nc.scalar.copy)):
-                    if first < last:
-                        copy(
-                            pairs[n][:, 2 * first : 2 * last].rearrange("p (c i j) -> p c j i", i=4, j=2),
-                            tile[:, :, first - lo : last - lo].rearrange("p j (c i) -> p c j i", i=4),
-                        )
+        def gather_into_place(e):
+            window = raw[LAST][-1][:, 0, :].indirect(offsets[:, e * C // 16 : (e + 1) * C // 16])
+            nc.vector.tensor_copy(woven_last[e][:, 3 : 4 * C : 4], window)
 
-        def gather(n, lo, hi):
-            g, u = divmod(n, 2)
-            nc.vector.tensor_copy(
-                picked[g][:, u, lo:hi], pairs[n][:].bitcast(U32).indirect(offsets[:, lo // 16 : hi // 16])
-            )
-
-        def weave(g, lo, hi, on_scalar):
-            dtype = U32 if on_scalar else I32
-            dst = woven_part(g, lo, hi).bitcast(dtype).rearrange("p (s u) -> p s u", u=2)
-            src = picked[g][:, :, lo:hi].bitcast(dtype).rearrange("p u s -> p s u")
-            (nc.scalar.copy if on_scalar else nc.vector.tensor_copy)(dst, src)
+        def weave(g, lo, hi, first, last, on_gpsimd=False):
+            dst = interleaved(g, lo, hi).rearrange("p (c i j) -> p c j i", i=4, j=4)
+            src = picked[g][:, :, lo:hi].rearrange("p j (c i) -> p c j i", i=4)
+            if on_gpsimd:
+                nc.gpsimd.tensor_scalar(
+                    interleaved(g, lo, hi).rearrange("p (s j) -> p s j", j=4),
+                    picked[g][:, :, lo:hi].rearrange("p j s -> p s j"),
+                    1.0,
+                    0.0,
+                    ALU.mult,
+                    ALU.add,
+                )
+            else:
+                nc.vector.tensor_copy(dst[:, :, first:last, :], src[:, :, first:last, :])
 
         def quantise(g, lo, hi):
             nc.vector.quantize_mx(
-                out=words[g][lo // (2 * C)][:, lo % (2 * C) : (hi - 1) % (2 * C) + 1].bitcast(FP8X4), scales=scales[g][:, lo:hi], in_=woven_part(g, lo, hi)
+                out=words[g][lo // HALF][:, lo % HALF : lo % HALF + hi - lo].bitcast(FP8X4), scales=scales[g][:, lo:hi], in_=interleaved(g, lo, hi)
             )
 
-        def multiply(g, e, start, stop):
+        def multiply(g, e):
             cols = slice(e * C, (e + 1) * C)
             if g < PASSES8:
                 lhs = w8[e // 2][:, e % 2 * PASSES8 + g, :].bitcast(FP8X4)
@@ -165,47 +165,52 @@ def tile_moe_res_lin_silu_kernel(
                 lhsT_scale=lhs_scale,
                 rhs=words[g][e // 2][:, e % 2 * C : (e % 2 + 1) * C].bitcast(FP8X4),
                 rhs_scale=scales[g][:, cols],
-                start=start,
-                stop=stop,
+                start=g == ORDER[e][0],
+                stop=g == ORDER[e][-1],
             )
 
-        half = SLOTS // 2
-        last = PASSES - 1
-        for g in range(PASSES):
-            round_pairs(2 * g)
+        for g in range(LAST):
+            gather(g, 0, 0, SLOTS, True)
+            gather(g, 1, 0, HALF, True)
+            gather(g, 1, HALF, SLOTS, False)
+            if g < LAST - 1:
+                for lo in (0, HALF):
+                    gather(g, 2, lo, lo + HALF, True)
+                    gather(g, 3, lo, lo + HALF, False)
+            else:
+                gather(g, 2, 0, SLOTS, False)
+                gather(g, 3, 0, HALF, True)
+                gather(g, 3, HALF, SLOTS, False)
+            weave(g, 0, HALF, 0, 4)
             if g > 0:
-                for lo in (0, C):
-                    weave(g - 1, lo, lo + C, False)
-                for lo in (0, C):
-                    quantise(g - 1, lo, lo + C)
-                if g < last:
-                    weave(g - 1, half, SLOTS, True)
-            gather(2 * g, 0, SLOTS)
-            if 0 < g < last:
-                quantise(g - 1, half, SLOTS)
-            round_pairs(2 * g + 1)
-            if g < last:
-                for lo in (0, half):
-                    gather(2 * g + 1, lo, lo + half)
-        weave(last - 1, half, SLOTS, True)
+                quantise(g - 1, HALF, SLOTS)
+            if g < LAST - 1:
+                quantise(g, 0, HALF)
+                weave(g, HALF, SLOTS, 0, 4, True)
+        weave(LAST - 1, HALF, SLOTS, 0, 4)
+        quantise(LAST - 1, 0, HALF)
+        gather(LAST, 0, 0, SLOTS, True)
+        gather(LAST, 1, 0, HALF, False)
+        gather(LAST, 1, HALF, SLOTS, True)
+        quantise(LAST - 1, HALF, SLOTS)
+        for e in (0, 1):
+            gather(LAST, 2, e * C, (e + 1) * C, True)
+        gather(LAST, 2, HALF, SLOTS, True)
+        for e in (0, 1):
+            weave(LAST, e * C, (e + 1) * C, 0, 3)
+        for e in (0, 1):
+            gather_into_place(e)
+        gather(LAST, 3, HALF, SLOTS, True)
+        for e in (0, 1):
+            quantise(LAST, e * C, (e + 1) * C)
+        for e in (2, 3):
+            weave(LAST, e * C, (e + 1) * C, 0, 4)
+        for e in (2, 3):
+            quantise(LAST, e * C, (e + 1) * C)
         for e in range(E):
-            gather(2 * last + 1, e * C, (e + 1) * C)
-        for e in range(E):
-            weave(last, e * C, (e + 1) * C, True)
-        for e in range(E):
-            if e == 2:
-                quantise(last - 1, half, SLOTS)
-            quantise(last, e * C, (e + 1) * C)
-        for h in range(2):
-            early = (2, 0, 1, last - 1) if h == 0 else (last - 1, 2)
-            late = (last,) if h == 0 else (last, 0, 1)
-            for g in early:
-                for e in (2 * h, 2 * h + 1):
-                    multiply(g, e, g == early[0], False)
-            for e in (2 * h, 2 * h + 1):
-                for g in late:
-                    multiply(g, e, False, g == late[-1])
-                nc.scalar.activation(y[:, e * C : (e + 1) * C], acc[e][:], ACT.Silu, bias=bias[:, e : e + 1])
+            for g in ORDER[e]:
+                multiply(g, e)
+            nc.scalar.activation(y[:, e * C : (e + 1) * C], acc[e][:], ACT.Silu, bias=bias[:, e : e + 1])
         for lo, hi in SCATTERS:
             nc.vector.tensor_tensor(
                 scattered[:].indirect(offsets[:, lo // 16 : hi // 16]), y[:, lo:hi], gates[:, lo:hi], ALU.mult

@@ -42,14 +42,17 @@ def tile_moe_res_lin_silu_kernel(
         raw = [[keep.tile([P, hi - lo, T], F32, name=f"raw{g}_{lo}", align_bytes=64) for lo, hi in LOADS[g]] for g in range(PASSES)]
         picked = [keep.tile([P, 4, SLOTS], F32, name=f"picked{g}") for g in range(PASSES)]
         woven = [
-            [keep.tile([P, 4 * HALF], BF16, name=f"woven{g}_{h}", tag=f"woven{g}" if g < LAST - 1 else f"woven{g}_{h}", align_bytes=64) for h in range(2)]
+            [keep.tile([P, 4 * HALF], BF16, name=f"woven{g}_{h}", align_bytes=64) for h in range(2)]
             for g in range(LAST)
         ]
+        woven_late = keep.tile([P, 4 * C], BF16, name="woven_late", tag=f"raw{LAST}_3", align_bytes=64)
         woven_last = [keep.tile([P, 4 * C], BF16, name=f"woven_last{e}", align_bytes=64) for e in range(E)]
 
         def interleaved(g, lo, hi):
             if g == LAST:
                 return woven_last[lo // C][:]
+            if g == LAST - 1 and lo == 3 * C:
+                return woven_late[:]
             return woven[g][lo // HALF][:, 4 * (lo % HALF) : 4 * (lo % HALF + hi - lo)]
 
         words = [
@@ -58,7 +61,6 @@ def tile_moe_res_lin_silu_kernel(
                     [P, HALF],
                     U32,
                     name=f"words{g}_{h}",
-                    tag=f"raw{g + 1}_{LOADS[g + 1][-1][0]}" if h == 1 and g < LAST - 1 else f"words{g}_{h}",
                     align_bytes=64,
                 )
                 for h in range(2)
@@ -89,15 +91,16 @@ def tile_moe_res_lin_silu_kernel(
         nc.scalar.dma_start(
             staged[0:P:8, E * PASSES8 :, :].bitcast(I32), w4_scales.rearrange("e a q n -> q (e a) n").bitcast(I32)
         )
+        nc.vector.memset(gate_rows[:], 0.0)
+        nc.gpsimd.dma_start(gate_rows[0:E, :], gate[0:1, :].rearrange("o (e c) -> (o e) c", e=E))
         nc.vector.memset(planes[:].bitcast(I32), 0)
         nc.gpsimd.dma_start(bias[:], b)
-        nc.vector.memset(gate_rows[:], 0.0)
         make_identity(nc, identity[:])
         nc.vector.memset(scattered[:], 0.0)
         for r in range(4):
             nc.gpsimd.dma_start(planes[r:P:32].bitcast(I32), staged[8 * r : P : 32].bitcast(I32))
         warm = keep.tile([P, 1], F32, name="warm")
-        nc.scalar.activation(warm[:], gate_rows[:, 0:1], ACT.Silu)
+        nc.scalar.activation(warm[:], scattered[:, 0:1], ACT.Silu)
 
         for g in range(PASSES):
             rows = xT[512 * g : 512 * (g + 1), :].rearrange("(p j) t -> p j t", j=4)
@@ -105,7 +108,6 @@ def tile_moe_res_lin_silu_kernel(
                 nc.sync.dma_start(tile[:], rows[:, lo:hi, :])
                 if g == 0 and lo == 0:
                     nc.sync.dma_start(offsets[:], offs)
-                    nc.sync.dma_start(gate_rows[0:E, :], gate[0:1, :].rearrange("o (e c) -> (o e) c", e=E))
         for h in range(2):
             nc.sync.dma_start(w4[h][:], w4_words[2 * h : 2 * h + 2].rearrange("e a p n -> p (e a) n"))
             nc.sync.dma_start(w8[h][:], w8_words[2 * h : 2 * h + 2].rearrange("e a p n r -> p (e a) (n r)"))
@@ -131,7 +133,7 @@ def tile_moe_res_lin_silu_kernel(
             window = raw[LAST][-1][:, 0, :].indirect(offsets[:, e * C // 16 : (e + 1) * C // 16])
             nc.vector.tensor_copy(woven_last[e][:, 3 : 4 * C : 4], window)
 
-        def weave(g, lo, hi, first, last, on_gpsimd=False):
+        def weave(g, lo, hi, first, last, on_gpsimd=False, on_scalar=False):
             dst = interleaved(g, lo, hi).rearrange("p (c i j) -> p c j i", i=4, j=4)
             src = picked[g][:, :, lo:hi].rearrange("p j (c i) -> p c j i", i=4)
             if on_gpsimd:
@@ -144,7 +146,8 @@ def tile_moe_res_lin_silu_kernel(
                     ALU.add,
                 )
             else:
-                nc.vector.tensor_copy(dst[:, :, first:last, :], src[:, :, first:last, :])
+                copy = nc.scalar.copy if on_scalar else nc.vector.tensor_copy
+                copy(dst[:, :, first:last, :], src[:, :, first:last, :])
 
         def quantise(g, lo, hi):
             nc.vector.quantize_mx(
@@ -182,17 +185,14 @@ def tile_moe_res_lin_silu_kernel(
                 gather(g, 3, 0, HALF, True)
                 gather(g, 3, HALF, SLOTS, False)
             weave(g, 0, HALF, 0, 4)
-            if g > 0:
-                quantise(g - 1, HALF, SLOTS)
+            weave(g, HALF, SLOTS if g < LAST - 1 else 3 * C, 0, 4)
+            quantise(g, 0, HALF)
             if g < LAST - 1:
-                quantise(g, 0, HALF)
-                weave(g, HALF, SLOTS, 0, 4, True)
-        weave(LAST - 1, HALF, SLOTS, 0, 4)
-        quantise(LAST - 1, 0, HALF)
+                quantise(g, HALF, SLOTS)
         gather(LAST, 0, 0, SLOTS, True)
         gather(LAST, 1, 0, HALF, False)
         gather(LAST, 1, HALF, SLOTS, True)
-        quantise(LAST - 1, HALF, SLOTS)
+        quantise(LAST - 1, HALF, 3 * C)
         for e in (0, 1):
             gather(LAST, 2, e * C, (e + 1) * C, True)
         gather(LAST, 2, HALF, SLOTS, True)
@@ -201,12 +201,14 @@ def tile_moe_res_lin_silu_kernel(
         for e in (0, 1):
             gather_into_place(e)
         gather(LAST, 3, HALF, SLOTS, True)
+        weave(LAST - 1, 3 * C, SLOTS, 0, 4, on_scalar=True)
         for e in (0, 1):
             quantise(LAST, e * C, (e + 1) * C)
         for e in (2, 3):
             weave(LAST, e * C, (e + 1) * C, 0, 4)
         for e in (2, 3):
             quantise(LAST, e * C, (e + 1) * C)
+        quantise(LAST - 1, 3 * C, SLOTS)
         for e in range(E):
             for g in ORDER[e]:
                 multiply(g, e)

@@ -74,28 +74,25 @@ def tile_moe_res_lin_silu_kernel(
         staged = keep.tile([P, E * PASSES, N], U8, name="staged", align_bytes=64)
         bias = keep.tile([P, E], F32, name="bias")
         identity = keep.tile([P, P], F32, name="identity")
-        gate_rows = keep.tile([P, C], F32, name="gate_rows")
         gate_columns = keep.tile([P, E], F32, name="gate_columns")
         gates = keep.tile([P, SLOTS], F32, name="gates")
         residual = keep.tile([P, T], F32, name="residual")
         y = keep.tile([P, SLOTS], F32, name="y")
         scattered = keep.tile([P, T], F32, name="scattered")
         result = keep.tile([P, T], F32, name="result")
-        turned = psum.tile([P, P], F32, name="turned")
         spread = psum.tile([P, SLOTS], F32, name="spread")
         acc = [psum.tile([P, C], F32, name=f"acc{e}") for e in range(E)]
 
+        nc.scalar.dma_start(gate_columns[:], gate[0:1, :].rearrange("o (m i) -> (o m) i", i=4))
         nc.scalar.dma_start(
             staged[0:P:8, 0 : E * PASSES8, :].bitcast(I32), w8_scales.rearrange("e a q n -> q (e a) n").bitcast(I32)
         )
         nc.scalar.dma_start(
             staged[0:P:8, E * PASSES8 :, :].bitcast(I32), w4_scales.rearrange("e a q n -> q (e a) n").bitcast(I32)
         )
-        nc.vector.memset(gate_rows[:], 0.0)
-        nc.gpsimd.dma_start(gate_rows[0:E, :], gate[0:1, :].rearrange("o (e c) -> (o e) c", e=E))
         nc.vector.memset(planes[:].bitcast(I32), 0)
-        nc.gpsimd.dma_start(bias[:], b)
         make_identity(nc, identity[:])
+        nc.gpsimd.dma_start(bias[:], b)
         nc.vector.memset(scattered[:], 0.0)
         for r in range(4):
             nc.gpsimd.dma_start(planes[r:P:32].bitcast(I32), staged[8 * r : P : 32].bitcast(I32))
@@ -113,13 +110,11 @@ def tile_moe_res_lin_silu_kernel(
             nc.sync.dma_start(w8[h][:], w8_words[2 * h : 2 * h + 2].rearrange("e a p n r -> p (e a) (n r)"))
         nc.sync.dma_start(residual[:], xr)
 
-        nc.tensor.transpose(turned[:], gate_rows[:], identity[:])
-        nc.scalar.copy(gate_columns[:], turned[:, 0:E])
-        for e in range(E):
+        for i in range(4):
             nc.tensor.transpose(
-                spread[:, e * C : (e + 1) * C], gate_columns[:, e : e + 1].to_broadcast([P, P]), identity[:]
+                spread[:, i * P : (i + 1) * P], gate_columns[:, i : i + 1].to_broadcast([P, P]), identity[:]
             )
-        nc.scalar.copy(gates[:], spread[:])
+        nc.scalar.copy(gates[:].rearrange("p (m i) -> p m i", i=4), spread[:].rearrange("p (i m) -> p m i", i=4))
 
         def gather(g, j, lo, hi, on_scalar):
             n = [first <= j < last for first, last in LOADS[g]].index(True)
@@ -217,6 +212,6 @@ def tile_moe_res_lin_silu_kernel(
             nc.vector.tensor_tensor(
                 scattered[:].indirect(offsets[:, lo // 16 : hi // 16]), y[:, lo:hi], gates[:, lo:hi], ALU.mult
             )
-        for n, (lo, hi) in enumerate(STORES):
+        for lo, hi in STORES:
             nc.vector.tensor_tensor(result[:, lo:hi], scattered[:, lo:hi], residual[:, lo:hi], ALU.add)
-            (nc.sync if n % 2 == 0 else nc.scalar).dma_start(out[:, lo:hi], result[:, lo:hi])
+            nc.sync.dma_start(out[:, lo:hi], result[:, lo:hi])

@@ -25,9 +25,8 @@ LAST = PASSES - 1
 FLOPS = 2 * K * SLOTS * N
 
 LOADS = (((0, 2), (2, 4)), ((0, 2), (2, 4)), ((0, 2), (2, 4)), ((0, 2), (2, 3), (3, 4)), ((0, 1), (1, 2), (2, 3), (3, 4)))
-ORDER = ((2, 3, 0, 1, 4), (2, 3, 0, 1, 4), (4, 2, 3, 0, 1), (4, 2, 3, 0, 1))
+GROUPS = ((0, 1), (1, 2), (2, 4))
 STORES = ((0, 256), (256, 640), (640, 1024))
-SCATTERS = ((0, 256), (256, 512))
 
 
 def tile_moe_res_lin_silu_kernel(
@@ -45,14 +44,14 @@ def tile_moe_res_lin_silu_kernel(
             [keep.tile([P, 4 * HALF], BF16, name=f"woven{g}_{h}", align_bytes=64) for h in range(2)]
             for g in range(LAST)
         ]
-        woven_late = keep.tile([P, 4 * C], BF16, name="woven_late", tag=f"raw{LAST}_3", align_bytes=64)
-        woven_last = [keep.tile([P, 4 * C], BF16, name=f"woven_last{e}", align_bytes=64) for e in range(E)]
+        woven_last = [
+            keep.tile([P, 4 * C], BF16, name=f"woven_last{e}", tag="w4_0" if e == 3 else f"woven_last{e}", align_bytes=64)
+            for e in range(E)
+        ]
 
         def interleaved(g, lo, hi):
             if g == LAST:
                 return woven_last[lo // C][:]
-            if g == LAST - 1 and lo == 3 * C:
-                return woven_late[:]
             return woven[g][lo // HALF][:, 4 * (lo % HALF) : 4 * (lo % HALF + hi - lo)]
 
         words = [
@@ -68,8 +67,8 @@ def tile_moe_res_lin_silu_kernel(
             for g in range(PASSES)
         ]
         scales = [keep.tile([P, SLOTS], U8, name=f"scales{g}", align_bytes=64) for g in range(PASSES)]
-        w8 = [keep.tile([P, 2 * PASSES8, 4 * N], U8, name=f"w8_{h}", align_bytes=64) for h in range(2)]
-        w4 = [keep.tile([P, 2 * PASSES4, 2 * N], U8, name=f"w4_{h}", align_bytes=64) for h in range(2)]
+        w8 = [keep.tile([P, (hi - lo) * PASSES8, 4 * N], U8, name=f"w8_{lo}", align_bytes=64) for lo, hi in GROUPS]
+        w4 = [keep.tile([P, (hi - lo) * PASSES4, 2 * N], U8, name=f"w4_{lo}", align_bytes=64) for lo, hi in GROUPS]
         planes = keep.tile([P, E * PASSES, N], U8, name="planes", align_bytes=64)
         staged = keep.tile([P, E * PASSES, N], U8, name="staged", align_bytes=64)
         bias = keep.tile([P, E], F32, name="bias")
@@ -81,7 +80,9 @@ def tile_moe_res_lin_silu_kernel(
         scattered = keep.tile([P, T], F32, name="scattered")
         result = keep.tile([P, T], F32, name="result")
         spread = psum.tile([P, SLOTS], F32, name="spread")
-        acc = [psum.tile([P, C], F32, name=f"acc{e}") for e in range(E)]
+        acc = [psum.tile([P, C], F32, name=f"acc{e}")[:] for e in range(2)]
+        acc_pair = psum.tile([P, 2 * C], F32, name="acc_pair")
+        acc.extend(acc_pair[:, i * C : (i + 1) * C] for i in range(2))
 
         nc.scalar.dma_start(gate_columns[:], gate[0:1, :].rearrange("o (m i) -> (o m) i", i=4))
         nc.scalar.dma_start(
@@ -105,9 +106,9 @@ def tile_moe_res_lin_silu_kernel(
                 nc.sync.dma_start(tile[:], rows[:, lo:hi, :])
                 if g == 0 and lo == 0:
                     nc.sync.dma_start(offsets[:], offs)
-        for h in range(2):
-            nc.sync.dma_start(w4[h][:], w4_words[2 * h : 2 * h + 2].rearrange("e a p n -> p (e a) n"))
-            nc.sync.dma_start(w8[h][:], w8_words[2 * h : 2 * h + 2].rearrange("e a p n r -> p (e a) (n r)"))
+        for n, (lo, hi) in enumerate(GROUPS):
+            nc.sync.dma_start(w4[n][:], w4_words[lo:hi].rearrange("e a p n -> p (e a) n"))
+            nc.sync.dma_start(w8[n][:], w8_words[lo:hi].rearrange("e a p n r -> p (e a) (n r)"))
         nc.sync.dma_start(residual[:], xr)
 
         for i in range(4):
@@ -124,9 +125,9 @@ def tile_moe_res_lin_silu_kernel(
             else:
                 nc.vector.tensor_copy(picked[g][:, j, lo:hi], window)
 
-        def gather_into_place(e):
-            window = raw[LAST][-1][:, 0, :].indirect(offsets[:, e * C // 16 : (e + 1) * C // 16])
-            nc.vector.tensor_copy(woven_last[e][:, 3 : 4 * C : 4], window)
+        def gather_into_place(j, e):
+            window = raw[LAST][j][:, 0, :].indirect(offsets[:, e * C // 16 : (e + 1) * C // 16])
+            nc.vector.tensor_copy(woven_last[e][:, j : 4 * C : 4], window)
 
         def weave(g, lo, hi, first, last, on_gpsimd=False, on_scalar=False):
             dst = interleaved(g, lo, hi).rearrange("p (c i j) -> p c j i", i=4, j=4)
@@ -149,22 +150,24 @@ def tile_moe_res_lin_silu_kernel(
                 out=words[g][lo // HALF][:, lo % HALF : lo % HALF + hi - lo].bitcast(FP8X4), scales=scales[g][:, lo:hi], in_=interleaved(g, lo, hi)
             )
 
-        def multiply(g, e):
+        def multiply(g, e, start, stop):
             cols = slice(e * C, (e + 1) * C)
+            n = [lo <= e < hi for lo, hi in GROUPS].index(True)
+            within = e - GROUPS[n][0]
             if g < PASSES8:
-                lhs = w8[e // 2][:, e % 2 * PASSES8 + g, :].bitcast(FP8X4)
+                lhs = w8[n][:, within * PASSES8 + g, :].bitcast(FP8X4)
                 lhs_scale = planes[:, e * PASSES8 + g, :]
             else:
-                lhs = w4[e // 2][:, e % 2 * PASSES4 + g - PASSES8, :].bitcast(FP4X4)
+                lhs = w4[n][:, within * PASSES4 + g - PASSES8, :].bitcast(FP4X4)
                 lhs_scale = planes[:, E * PASSES8 + e * PASSES4 + g - PASSES8, :]
             nc.tensor.matmul_mx(
-                out=acc[e][:],
+                out=acc[e],
                 lhsT=lhs,
                 lhsT_scale=lhs_scale,
                 rhs=words[g][e // 2][:, e % 2 * C : (e % 2 + 1) * C].bitcast(FP8X4),
                 rhs_scale=scales[g][:, cols],
-                start=g == ORDER[e][0],
-                stop=g == ORDER[e][-1],
+                start=start,
+                stop=stop,
             )
 
         for g in range(LAST):
@@ -180,38 +183,48 @@ def tile_moe_res_lin_silu_kernel(
                 gather(g, 3, 0, HALF, True)
                 gather(g, 3, HALF, SLOTS, False)
             weave(g, 0, HALF, 0, 4)
-            weave(g, HALF, SLOTS if g < LAST - 1 else 3 * C, 0, 4)
+            weave(g, HALF, SLOTS, 0, 4)
             quantise(g, 0, HALF)
             if g < LAST - 1:
                 quantise(g, HALF, SLOTS)
+        quantise(LAST - 1, HALF, SLOTS)
         gather(LAST, 0, 0, SLOTS, True)
-        gather(LAST, 1, 0, HALF, False)
-        gather(LAST, 1, HALF, SLOTS, True)
-        quantise(LAST - 1, HALF, 3 * C)
-        for e in (0, 1):
-            gather(LAST, 2, e * C, (e + 1) * C, True)
-        gather(LAST, 2, HALF, SLOTS, True)
-        for e in (0, 1):
-            weave(LAST, e * C, (e + 1) * C, 0, 3)
-        for e in (0, 1):
-            gather_into_place(e)
+        for lo in (0, HALF):
+            gather(LAST, 1, lo, lo + HALF, True)
+        weave(LAST, 0, C, 0, 2)
+        gather_into_place(2, 0)
+        gather(LAST, 2, C, SLOTS, True)
+        gather_into_place(3, 0)
+        gather(LAST, 3, C, HALF, True)
         gather(LAST, 3, HALF, SLOTS, True)
-        weave(LAST - 1, 3 * C, SLOTS, 0, 4, on_scalar=True)
-        for e in (0, 1):
+        quantise(LAST, 0, C)
+        weave(LAST, C, HALF, 0, 4)
+        weave(LAST, HALF, 3 * C, 0, 4)
+        for e in (1, 2):
             quantise(LAST, e * C, (e + 1) * C)
-        for e in (2, 3):
-            weave(LAST, e * C, (e + 1) * C, 0, 4)
-        for e in (2, 3):
-            quantise(LAST, e * C, (e + 1) * C)
-        quantise(LAST - 1, 3 * C, SLOTS)
-        for e in range(E):
-            for g in ORDER[e]:
-                multiply(g, e)
-            nc.scalar.activation(y[:, e * C : (e + 1) * C], acc[e][:], ACT.Silu, bias=bias[:, e : e + 1])
-        for lo, hi in SCATTERS:
+
+        def silu(e):
+            nc.scalar.activation(y[:, e * C : (e + 1) * C], acc[e], ACT.Silu, bias=bias[:, e : e + 1])
+
+        def scatter(lo, hi):
             nc.vector.tensor_tensor(
                 scattered[:].indirect(offsets[:, lo // 16 : hi // 16]), y[:, lo:hi], gates[:, lo:hi], ALU.mult
             )
+
+        for e in (0, 1):
+            for g in (2, 3, 0, 1, 4):
+                multiply(g, e, g == 2, g == 4)
+            silu(e)
+            scatter(e * C, (e + 1) * C)
+            if e == 0:
+                weave(LAST, 3 * C, SLOTS, 0, 4, on_scalar=True)
+                quantise(LAST, 3 * C, SLOTS)
+        steps = [(g, e) for g in (2, 3, 0, 1, 4) for e in (2, 3)]
+        for g, e in steps:
+            multiply(g, e, (g, e) == steps[0], (g, e) == steps[-1])
+        for e in (2, 3):
+            silu(e)
+        scatter(HALF, SLOTS)
         for lo, hi in STORES:
             nc.vector.tensor_tensor(result[:, lo:hi], scattered[:, lo:hi], residual[:, lo:hi], ALU.add)
             nc.sync.dma_start(out[:, lo:hi], result[:, lo:hi])

@@ -25,7 +25,6 @@ LAST = PASSES - 1
 FLOPS = 2 * K * SLOTS * N
 
 LOADS = (((0, 2), (2, 4)), ((0, 2), (2, 4)), ((0, 2), (2, 4)), ((0, 2), (2, 3), (3, 4)), ((0, 1), (1, 2), (2, 3), (3, 4)))
-GROUPS = ((0, 1), (1, 2), (2, 4))
 STORES = ((0, 256), (256, 640), (640, 1024))
 
 
@@ -44,31 +43,17 @@ def tile_moe_res_lin_silu_kernel(
             [keep.tile([P, 4 * HALF], BF16, name=f"woven{g}_{h}", align_bytes=64) for h in range(2)]
             for g in range(LAST)
         ]
-        woven_last = [
-            keep.tile([P, 4 * C], BF16, name=f"woven_last{e}", tag="w4_0" if e == 3 else f"woven_last{e}", align_bytes=64)
-            for e in range(E)
+        woven_last = [keep.tile([P, 4 * C], BF16, name=f"woven_last{e}", align_bytes=64) for e in range(E - 1)]
+        woven_end = [
+            keep.tile([P, 2 * C], BF16, name=f"woven_end{h}", tag="w4_0" if h == 1 else "woven_end0", align_bytes=64)
+            for h in range(2)
         ]
-
-        def interleaved(g, lo, hi):
-            if g == LAST:
-                return woven_last[lo // C][:]
-            return woven[g][lo // HALF][:, 4 * (lo % HALF) : 4 * (lo % HALF + hi - lo)]
-
-        words = [
-            [
-                keep.tile(
-                    [P, HALF],
-                    U32,
-                    name=f"words{g}_{h}",
-                    align_bytes=64,
-                )
-                for h in range(2)
-            ]
-            for g in range(PASSES)
-        ]
-        scales = [keep.tile([P, SLOTS], U8, name=f"scales{g}", align_bytes=64) for g in range(PASSES)]
-        w8 = [keep.tile([P, (hi - lo) * PASSES8, 4 * N], U8, name=f"w8_{lo}", align_bytes=64) for lo, hi in GROUPS]
-        w4 = [keep.tile([P, (hi - lo) * PASSES4, 2 * N], U8, name=f"w4_{lo}", align_bytes=64) for lo, hi in GROUPS]
+        words = [[keep.tile([P, HALF], U32, name=f"words{g}_{h}", align_bytes=64) for h in range(2)] for g in range(LAST)]
+        scales = [keep.tile([P, SLOTS], U8, name=f"scales{g}", align_bytes=64) for g in range(LAST)]
+        words_last = [keep.tile([P, C], U32, name=f"words_last{e}", align_bytes=64) for e in range(E)]
+        scales_last = [keep.tile([P, C], U8, name=f"scales_last{e}", align_bytes=64) for e in range(E)]
+        w8 = [keep.tile([P, PASSES8, 4 * N], U8, name=f"w8_{e}", align_bytes=64) for e in range(E)]
+        w4 = [keep.tile([P, PASSES4, 2 * N], U8, name=f"w4_{e}", align_bytes=64) for e in range(E)]
         planes = keep.tile([P, E * PASSES, N], U8, name="planes", align_bytes=64)
         staged = keep.tile([P, E * PASSES, N], U8, name="staged", align_bytes=64)
         bias = keep.tile([P, E], F32, name="bias")
@@ -76,13 +61,26 @@ def tile_moe_res_lin_silu_kernel(
         gate_columns = keep.tile([P, E], F32, name="gate_columns")
         gates = keep.tile([P, SLOTS], F32, name="gates")
         residual = keep.tile([P, T], F32, name="residual")
-        y = keep.tile([P, SLOTS], F32, name="y")
-        scattered = keep.tile([P, T], F32, name="scattered")
+        y = [keep.tile([P, C], F32, name=f"y{e}") for e in range(E)]
+        gated = [keep.tile([P, C], F32, name=f"gated{e}", tag="w4_2" if e == 1 else "gated3", align_bytes=64) for e in (1, 3)]
+        windows = [keep.tile([P, T], F32, name=f"window{i}") for i in range(2)]
+        partial = keep.tile([P, T], F32, name="partial")
         result = keep.tile([P, T], F32, name="result")
         spread = psum.tile([P, SLOTS], F32, name="spread")
-        acc = [psum.tile([P, C], F32, name=f"acc{e}")[:] for e in range(2)]
-        acc_pair = psum.tile([P, 2 * C], F32, name="acc_pair")
-        acc.extend(acc_pair[:, i * C : (i + 1) * C] for i in range(2))
+        acc = [psum.tile([P, C], F32, name=f"acc{e}", tag=f"acc{1 if e == 3 else e}") for e in range(E)]
+
+        def codes(g, lo, hi):
+            if g == LAST:
+                cols = slice(lo % C, lo % C + hi - lo)
+                return words_last[lo // C][:, cols].bitcast(FP8X4), scales_last[lo // C][:, cols]
+            return words[g][lo // HALF][:, lo % HALF : lo % HALF + hi - lo].bitcast(FP8X4), scales[g][:, lo:hi]
+
+        def interleaved(g, lo, hi):
+            if g == LAST and lo >= 3 * C:
+                return woven_end[(lo - 3 * C) // (C // 2)][:]
+            if g == LAST:
+                return woven_last[lo // C][:]
+            return woven[g][lo // HALF][:, 4 * (lo % HALF) : 4 * (lo % HALF + hi - lo)]
 
         nc.scalar.dma_start(gate_columns[:], gate[0:1, :].rearrange("o (m i) -> (o m) i", i=4))
         nc.scalar.dma_start(
@@ -94,11 +92,12 @@ def tile_moe_res_lin_silu_kernel(
         nc.vector.memset(planes[:].bitcast(I32), 0)
         make_identity(nc, identity[:])
         nc.gpsimd.dma_start(bias[:], b)
-        nc.vector.memset(scattered[:], 0.0)
+        for window in windows:
+            nc.vector.memset(window[:], 0.0)
         for r in range(4):
             nc.gpsimd.dma_start(planes[r:P:32].bitcast(I32), staged[8 * r : P : 32].bitcast(I32))
         warm = keep.tile([P, 1], F32, name="warm")
-        nc.scalar.activation(warm[:], scattered[:, 0:1], ACT.Silu)
+        nc.scalar.activation(warm[:], windows[0][:, 0:1], ACT.Silu)
 
         for g in range(PASSES):
             rows = xT[512 * g : 512 * (g + 1), :].rearrange("(p j) t -> p j t", j=4)
@@ -106,9 +105,9 @@ def tile_moe_res_lin_silu_kernel(
                 nc.sync.dma_start(tile[:], rows[:, lo:hi, :])
                 if g == 0 and lo == 0:
                     nc.sync.dma_start(offsets[:], offs)
-        for n, (lo, hi) in enumerate(GROUPS):
-            nc.sync.dma_start(w4[n][:], w4_words[lo:hi].rearrange("e a p n -> p (e a) n"))
-            nc.sync.dma_start(w8[n][:], w8_words[lo:hi].rearrange("e a p n r -> p (e a) (n r)"))
+        for e in range(E):
+            nc.sync.dma_start(w4[e][:], w4_words[e].rearrange("a p n -> p a n"))
+            nc.sync.dma_start(w8[e][:], w8_words[e].rearrange("a p n r -> p a (n r)"))
         nc.sync.dma_start(residual[:], xr)
 
         for i in range(4):
@@ -129,43 +128,30 @@ def tile_moe_res_lin_silu_kernel(
             window = raw[LAST][j][:, 0, :].indirect(offsets[:, e * C // 16 : (e + 1) * C // 16])
             nc.vector.tensor_copy(woven_last[e][:, j : 4 * C : 4], window)
 
-        def weave(g, lo, hi, first, last, on_gpsimd=False, on_scalar=False):
+        def weave(g, lo, hi, first, last, on_scalar=False):
             dst = interleaved(g, lo, hi).rearrange("p (c i j) -> p c j i", i=4, j=4)
             src = picked[g][:, :, lo:hi].rearrange("p j (c i) -> p c j i", i=4)
-            if on_gpsimd:
-                nc.gpsimd.tensor_scalar(
-                    interleaved(g, lo, hi).rearrange("p (s j) -> p s j", j=4),
-                    picked[g][:, :, lo:hi].rearrange("p j s -> p s j"),
-                    1.0,
-                    0.0,
-                    ALU.mult,
-                    ALU.add,
-                )
-            else:
-                copy = nc.scalar.copy if on_scalar else nc.vector.tensor_copy
-                copy(dst[:, :, first:last, :], src[:, :, first:last, :])
+            copy = nc.scalar.copy if on_scalar else nc.vector.tensor_copy
+            copy(dst[:, :, first:last, :], src[:, :, first:last, :])
 
         def quantise(g, lo, hi):
-            nc.vector.quantize_mx(
-                out=words[g][lo // HALF][:, lo % HALF : lo % HALF + hi - lo].bitcast(FP8X4), scales=scales[g][:, lo:hi], in_=interleaved(g, lo, hi)
-            )
+            packed, exponents = codes(g, lo, hi)
+            nc.vector.quantize_mx(out=packed, scales=exponents, in_=interleaved(g, lo, hi))
 
         def multiply(g, e, start, stop):
-            cols = slice(e * C, (e + 1) * C)
-            n = [lo <= e < hi for lo, hi in GROUPS].index(True)
-            within = e - GROUPS[n][0]
             if g < PASSES8:
-                lhs = w8[n][:, within * PASSES8 + g, :].bitcast(FP8X4)
+                lhs = w8[e][:, g, :].bitcast(FP8X4)
                 lhs_scale = planes[:, e * PASSES8 + g, :]
             else:
-                lhs = w4[n][:, within * PASSES4 + g - PASSES8, :].bitcast(FP4X4)
+                lhs = w4[e][:, g - PASSES8, :].bitcast(FP4X4)
                 lhs_scale = planes[:, E * PASSES8 + e * PASSES4 + g - PASSES8, :]
+            packed, exponents = codes(g, e * C, (e + 1) * C)
             nc.tensor.matmul_mx(
-                out=acc[e],
+                out=acc[e][:],
                 lhsT=lhs,
                 lhsT_scale=lhs_scale,
-                rhs=words[g][e // 2][:, e % 2 * C : (e % 2 + 1) * C].bitcast(FP8X4),
-                rhs_scale=scales[g][:, cols],
+                rhs=packed,
+                rhs_scale=exponents,
                 start=start,
                 stop=stop,
             )
@@ -185,46 +171,48 @@ def tile_moe_res_lin_silu_kernel(
             weave(g, 0, HALF, 0, 4)
             weave(g, HALF, SLOTS, 0, 4)
             quantise(g, 0, HALF)
-            if g < LAST - 1:
-                quantise(g, HALF, SLOTS)
-        quantise(LAST - 1, HALF, SLOTS)
+            quantise(g, HALF, SLOTS)
         gather(LAST, 0, 0, SLOTS, True)
-        for lo in (0, HALF):
-            gather(LAST, 1, lo, lo + HALF, True)
+        gather(LAST, 1, 0, HALF, True)
+        gather(LAST, 1, HALF, SLOTS, False)
         weave(LAST, 0, C, 0, 2)
         gather_into_place(2, 0)
         gather(LAST, 2, C, SLOTS, True)
         gather_into_place(3, 0)
         gather(LAST, 3, C, HALF, True)
         gather(LAST, 3, HALF, SLOTS, True)
-        quantise(LAST, 0, C)
         weave(LAST, C, HALF, 0, 4)
+        quantise(LAST, 0, C)
         weave(LAST, HALF, 3 * C, 0, 4)
         for e in (1, 2):
             quantise(LAST, e * C, (e + 1) * C)
 
-        def silu(e):
-            nc.scalar.activation(y[:, e * C : (e + 1) * C], acc[e], ACT.Silu, bias=bias[:, e : e + 1])
-
-        def scatter(lo, hi):
-            nc.vector.tensor_tensor(
-                scattered[:].indirect(offsets[:, lo // 16 : hi // 16]), y[:, lo:hi], gates[:, lo:hi], ALU.mult
-            )
-
-        for e in (0, 1):
+        def activate(e):
             for g in (2, 3, 0, 1, 4):
                 multiply(g, e, g == 2, g == 4)
-            silu(e)
-            scatter(e * C, (e + 1) * C)
-            if e == 0:
-                weave(LAST, 3 * C, SLOTS, 0, 4, on_scalar=True)
-                quantise(LAST, 3 * C, SLOTS)
-        steps = [(g, e) for g in (2, 3, 0, 1, 4) for e in (2, 3)]
-        for g, e in steps:
-            multiply(g, e, (g, e) == steps[0], (g, e) == steps[-1])
-        for e in (2, 3):
-            silu(e)
-        scatter(HALF, SLOTS)
+            nc.scalar.activation(y[e][:], acc[e][:], ACT.Silu, bias=bias[:, e : e + 1])
+
+        def places(e):
+            return windows[e % 2][:].indirect(offsets[:, e * C // 16 : (e + 1) * C // 16])
+
+        def times_gate(dst, e):
+            nc.vector.tensor_tensor(dst, y[e][:], gates[:, e * C : (e + 1) * C], ALU.mult)
+
+        activate(0)
+        times_gate(places(0), 0)
+        for lo in (3 * C, 3 * C + C // 2):
+            weave(LAST, lo, lo + C // 2, 0, 4, on_scalar=True)
+            quantise(LAST, lo, lo + C // 2)
+        activate(1)
+        times_gate(gated[0][:], 1)
+        activate(2)
+        nc.scalar.activation(places(1), gated[0][:], ACT.Copy)
+        times_gate(places(2), 2)
+        activate(3)
+        times_gate(gated[1][:], 3)
+        nc.scalar.activation(places(3), gated[1][:], ACT.Copy)
         for lo, hi in STORES:
-            nc.vector.tensor_tensor(result[:, lo:hi], scattered[:, lo:hi], residual[:, lo:hi], ALU.add)
+            nc.vector.tensor_tensor(partial[:, lo:hi], windows[0][:, lo:hi], residual[:, lo:hi], ALU.add)
+        for lo, hi in STORES:
+            nc.vector.tensor_tensor(result[:, lo:hi], windows[1][:, lo:hi], partial[:, lo:hi], ALU.add)
             nc.sync.dma_start(out[:, lo:hi], result[:, lo:hi])

from contextlib import ExitStack

import concourse.mybir as mybir
from concourse.masks import make_identity

F32 = mybir.dt.float32
BF16 = mybir.dt.bfloat16
U32 = mybir.dt.uint32
I32 = mybir.dt.int32
U16 = mybir.dt.uint16
U8 = mybir.dt.uint8
FP8X4 = mybir.dt.float8_e4m3fn_x4
FP4X4 = mybir.dt.float4_e2m1fn_x4
ACT = mybir.ActivationFunctionType
ALU = mybir.AluOpType

P = 128
K, T, E, C, N = 2560, 1024, 4, 128, 128
PASSES8, PASSES4 = 2, 3
PASSES = PASSES8 + PASSES4
SLOTS = E * C
HALF = SLOTS // 2
LAST = PASSES - 1

FLOPS = 2 * K * SLOTS * N

LOADS = (((0, 2), (2, 4)), ((0, 2), (2, 4)), ((0, 2), (2, 4)), ((0, 2), (2, 3), (3, 4)), ((0, 1), (1, 2), (2, 3), (3, 4)))
STORES = ((0, 256), (256, 640), (640, 1024))


def tile_moe_res_lin_silu_kernel(
    tc, xT, xr, w8_words, w8_scales, w4_words, w4_scales, b, gate, offs, out
):
    nc = tc.nc
    with ExitStack() as ctx:
        keep = ctx.enter_context(tc.tile_pool(name="keep", bufs=1))
        psum = ctx.enter_context(tc.psum_pool(name="psum", bufs=1))

        offsets = keep.tile([P, SLOTS // 16], U16, name="offsets")
        raw = [[keep.tile([P, hi - lo, T], F32, name=f"raw{g}_{lo}", align_bytes=64) for lo, hi in LOADS[g]] for g in range(PASSES)]
        picked = [keep.tile([P, 4, SLOTS], F32, name=f"picked{g}") for g in range(PASSES)]
        woven = [
            [keep.tile([P, 4 * HALF], BF16, name=f"woven{g}_{h}", align_bytes=64) for h in range(2)]
            for g in range(LAST)
        ]
        woven_last = [keep.tile([P, 4 * C], BF16, name=f"woven_last{e}", align_bytes=64) for e in range(E - 1)]
        woven_end = [
            keep.tile([P, 2 * C], BF16, name=f"woven_end{h}", tag="w4_0" if h == 1 else "woven_end0", align_bytes=64)
            for h in range(2)
        ]
        words = [[keep.tile([P, HALF], U32, name=f"words{g}_{h}", align_bytes=64) for h in range(2)] for g in range(LAST)]
        scales = [keep.tile([P, SLOTS], U8, name=f"scales{g}", align_bytes=64) for g in range(LAST)]
        words_last = [keep.tile([P, C], U32, name=f"words_last{e}", align_bytes=64) for e in range(E)]
        scales_last = [keep.tile([P, C], U8, name=f"scales_last{e}", align_bytes=64) for e in range(E)]
        w8 = [keep.tile([P, PASSES8, 4 * N], U8, name=f"w8_{e}", align_bytes=64) for e in range(E)]
        w4 = [keep.tile([P, PASSES4, 2 * N], U8, name=f"w4_{e}", align_bytes=64) for e in range(E)]
        planes = keep.tile([P, E * PASSES, N], U8, name="planes", align_bytes=64)
        staged = keep.tile([P, E * PASSES, N], U8, name="staged", align_bytes=64)
        bias = keep.tile([P, E], F32, name="bias")
        identity = keep.tile([P, P], F32, name="identity")
        gate_columns = keep.tile([P, E], F32, name="gate_columns")
        gates = keep.tile([P, SLOTS], F32, name="gates")
        residual = keep.tile([P, T], F32, name="residual")
        y = [keep.tile([P, C], F32, name=f"y{e}") for e in range(E)]
        gated = [keep.tile([P, C], F32, name=f"gated{e}", tag="w4_2" if e == 1 else "gated3", align_bytes=64) for e in (1, 3)]
        windows = [keep.tile([P, T], F32, name=f"window{i}") for i in range(2)]
        partial = keep.tile([P, T], F32, name="partial")
        result = keep.tile([P, T], F32, name="result")
        spread = psum.tile([P, SLOTS], F32, name="spread")
        acc = [psum.tile([P, C], F32, name=f"acc{e}", tag=f"acc{1 if e == 3 else e}") for e in range(E)]

        def codes(g, lo, hi):
            if g == LAST:
                cols = slice(lo % C, lo % C + hi - lo)
                return words_last[lo // C][:, cols].bitcast(FP8X4), scales_last[lo // C][:, cols]
            return words[g][lo // HALF][:, lo % HALF : lo % HALF + hi - lo].bitcast(FP8X4), scales[g][:, lo:hi]

        def interleaved(g, lo, hi):
            if g == LAST and lo >= 3 * C:
                return woven_end[(lo - 3 * C) // (C // 2)][:]
            if g == LAST:
                return woven_last[lo // C][:]
            return woven[g][lo // HALF][:, 4 * (lo % HALF) : 4 * (lo % HALF + hi - lo)]

        nc.scalar.dma_start(gate_columns[:], gate[0:1, :].rearrange("o (m i) -> (o m) i", i=4))
        nc.scalar.dma_start(
            staged[0:P:8, 0 : E * PASSES8, :].bitcast(I32), w8_scales.rearrange("e a q n -> q (e a) n").bitcast(I32)
        )
        nc.scalar.dma_start(
            staged[0:P:8, E * PASSES8 :, :].bitcast(I32), w4_scales.rearrange("e a q n -> q (e a) n").bitcast(I32)
        )
        nc.vector.memset(planes[:].bitcast(I32), 0)
        make_identity(nc, identity[:])
        nc.gpsimd.dma_start(bias[:], b)
        for window in windows:
            nc.vector.memset(window[:], 0.0)
        for r in range(4):
            nc.gpsimd.dma_start(planes[r:P:32].bitcast(I32), staged[8 * r : P : 32].bitcast(I32))
        warm = keep.tile([P, 1], F32, name="warm")
        nc.scalar.activation(warm[:], windows[0][:, 0:1], ACT.Silu)

        for g in range(PASSES):
            rows = xT[512 * g : 512 * (g + 1), :].rearrange("(p j) t -> p j t", j=4)
            for (lo, hi), tile in zip(LOADS[g], raw[g]):
                nc.sync.dma_start(tile[:], rows[:, lo:hi, :])
                if g == 0 and lo == 0:
                    nc.sync.dma_start(offsets[:], offs)
        for e in range(E):
            nc.sync.dma_start(w4[e][:], w4_words[e].rearrange("a p n -> p a n"))
            nc.sync.dma_start(w8[e][:], w8_words[e].rearrange("a p n r -> p a (n r)"))
        nc.sync.dma_start(residual[:], xr)

        for i in range(4):
            nc.tensor.transpose(
                spread[:, i * P : (i + 1) * P], gate_columns[:, i : i + 1].to_broadcast([P, P]), identity[:]
            )
        nc.scalar.copy(gates[:].rearrange("p (m i) -> p m i", i=4), spread[:].rearrange("p (i m) -> p m i", i=4))

        def gather(g, j, lo, hi, on_scalar):
            n = [first <= j < last for first, last in LOADS[g]].index(True)
            window = raw[g][n][:, j - LOADS[g][n][0], :].indirect(offsets[:, lo // 16 : hi // 16])
            if on_scalar:
                nc.scalar.activation(picked[g][:, j, lo:hi], window, ACT.Copy)
            else:
                nc.vector.tensor_copy(picked[g][:, j, lo:hi], window)

        def gather_into_place(j, e):
            window = raw[LAST][j][:, 0, :].indirect(offsets[:, e * C // 16 : (e + 1) * C // 16])
            nc.vector.tensor_copy(woven_last[e][:, j : 4 * C : 4], window)

        def weave(g, lo, hi, first, last, on_scalar=False):
            dst = interleaved(g, lo, hi).rearrange("p (c i j) -> p c j i", i=4, j=4)
            src = picked[g][:, :, lo:hi].rearrange("p j (c i) -> p c j i", i=4)
            copy = nc.scalar.copy if on_scalar else nc.vector.tensor_copy
            copy(dst[:, :, first:last, :], src[:, :, first:last, :])

        def quantise(g, lo, hi):
            packed, exponents = codes(g, lo, hi)
            nc.vector.quantize_mx(out=packed, scales=exponents, in_=interleaved(g, lo, hi))

        def multiply(g, e, start, stop):
            if g < PASSES8:
                lhs = w8[e][:, g, :].bitcast(FP8X4)
                lhs_scale = planes[:, e * PASSES8 + g, :]
            else:
                lhs = w4[e][:, g - PASSES8, :].bitcast(FP4X4)
                lhs_scale = planes[:, E * PASSES8 + e * PASSES4 + g - PASSES8, :]
            packed, exponents = codes(g, e * C, (e + 1) * C)
            nc.tensor.matmul_mx(
                out=acc[e][:],
                lhsT=lhs,
                lhsT_scale=lhs_scale,
                rhs=packed,
                rhs_scale=exponents,
                start=start,
                stop=stop,
            )

        for g in range(LAST):
            gather(g, 0, 0, SLOTS, True)
            gather(g, 1, 0, HALF, True)
            gather(g, 1, HALF, SLOTS, False)
            if g < LAST - 1:
                for lo in (0, HALF):
                    gather(g, 2, lo, lo + HALF, True)
                    gather(g, 3, lo, lo + HALF, False)
            else:
                gather(g, 2, 0, SLOTS, False)
                gather(g, 3, 0, HALF, True)
                gather(g, 3, HALF, SLOTS, False)
            weave(g, 0, HALF, 0, 4)
            weave(g, HALF, SLOTS, 0, 4)
            quantise(g, 0, HALF)
            quantise(g, HALF, SLOTS)
        gather(LAST, 0, 0, SLOTS, True)
        gather(LAST, 1, 0, HALF, True)
        gather(LAST, 1, HALF, SLOTS, False)
        weave(LAST, 0, C, 0, 2)
        gather_into_place(2, 0)
        gather(LAST, 2, C, SLOTS, True)
        gather_into_place(3, 0)
        gather(LAST, 3, C, HALF, True)
        gather(LAST, 3, HALF, SLOTS, True)
        weave(LAST, C, HALF, 0, 4)
        quantise(LAST, 0, C)
        weave(LAST, HALF, 3 * C, 0, 4)
        for e in (1, 2):
            quantise(LAST, e * C, (e + 1) * C)

        def activate(e):
            for g in (2, 3, 0, 1, 4):
                multiply(g, e, g == 2, g == 4)
            nc.scalar.activation(y[e][:], acc[e][:], ACT.Silu, bias=bias[:, e : e + 1])

        def places(e):
            return windows[e % 2][:].indirect(offsets[:, e * C // 16 : (e + 1) * C // 16])

        def times_gate(dst, e):
            nc.vector.tensor_tensor(dst, y[e][:], gates[:, e * C : (e + 1) * C], ALU.mult)

        activate(0)
        times_gate(places(0), 0)
        for lo in (3 * C, 3 * C + C // 2):
            weave(LAST, lo, lo + C // 2, 0, 4, on_scalar=True)
            quantise(LAST, lo, lo + C // 2)
        activate(1)
        times_gate(gated[0][:], 1)
        activate(2)
        nc.scalar.activation(places(1), gated[0][:], ACT.Copy)
        times_gate(places(2), 2)
        activate(3)
        times_gate(gated[1][:], 3)
        nc.scalar.activation(places(3), gated[1][:], ACT.Copy)
        for lo, hi in STORES:
            nc.vector.tensor_tensor(partial[:, lo:hi], windows[0][:, lo:hi], residual[:, lo:hi], ALU.add)
        for lo, hi in STORES:
            nc.vector.tensor_tensor(result[:, lo:hi], windows[1][:, lo:hi], partial[:, lo:hi], ALU.add)
            nc.sync.dma_start(out[:, lo:hi], result[:, lo:hi])
